import numpy as np, ml_dtypes
CORES = [36,164,52,180,100,228,116,244]
N = 8
import mx_ref
BF = ml_dtypes.bfloat16
def gentries(a):
    return np.ascontiguousarray(a.reshape(8, 16, -1).transpose(0, 2, 1)).reshape(8, -1)
def gtable(e):
    e = np.asarray(e); return np.ascontiguousarray(e.reshape(8, -1, 16).transpose(0, 2, 1)).reshape(128, -1).astype(np.int32)
def gcols(t, e):
    v = np.concatenate([t.reshape(8, 16, -1, 4), np.zeros((8, 16, 1, 4), BF)], axis=2)
    return np.ascontiguousarray(np.stack([v[g][:, e[g]] for g in range(8)])).reshape(128, -1)
def gpick(z, e):
    return np.concatenate([z[16 * g:16 * g + 16][:, e[g]] for g in range(8)])
def tile(rs):
    return np.stack(rs, axis=2).reshape(128, -1).astype(BF)
def pick(q, e):
    c = np.concatenate([q[0].reshape(128, -1, 4), np.zeros((128, 1, 4), np.uint8)], axis=1); s = np.concatenate([q[1], np.ones((16, 1), np.uint8)], axis=1)
    return (np.ascontiguousarray(c[:, e].reshape(128, -1)), np.ascontiguousarray(s[:, e]))
def join(*qs):
    return (np.concatenate([q[0] for q in qs], axis=1), np.concatenate([q[1] for q in qs], axis=1))
def put(q, e, v):
    c, s = q[0].reshape(128, -1, 4).copy(), q[1].copy(); c[:, e] = v[0].reshape(128, -1, 4); s[:, e] = v[1]
    return (c.reshape(128, -1), s)
def pk(c, s):
    return (np.ascontiguousarray(c), mx_ref.live(s))
def emit(q):
    return q[0], q[1]
def packed(v, rng):
    q = [mx_ref.quantize(np.ascontiguousarray(v[r])) for r in range(N)]
    return np.stack([a for a, b in q]), np.stack([mx_ref.plane(b, rng) for a, b in q])
def values_of_codes():
    e, c = np.zeros((128, 128, 4), np.float32), np.zeros((128, 2, 4), np.uint8)
    e[np.arange(128), np.arange(128), 0] = 1
    c[:127, :, 0] = np.arange(256).reshape(2, 128).T[:127]
    return mx_ref.matmul(mx_ref.quantize(e.reshape(128, 512).astype(BF)), (c.reshape(128, 8), np.full((16, 2), 127, np.uint8))).T.reshape(-1).astype(np.float64)
CODE_VALUE, SCALE_VALUE = values_of_codes(), 2.0 ** (np.arange(256) - 127.0)
def decode(q):
    return (CODE_VALUE[q[0]].reshape(16, 8, -1, 4) * SCALE_VALUE[q[1]][:, None, :, None] + 0.0).reshape(128, -1).astype(np.float32)
def f(rng, *shape):
    return mx_ref.flush((rng.standard_normal(shape, dtype=np.float32) * np.exp2(rng.integers(-2, 3, shape[:-1] + (1,)))).astype(BF))
def wide(rng, *shape, cols=0):
    v = rng.standard_normal(shape, dtype=np.float32) * np.exp2(rng.integers(-12, 13, shape)).astype(np.float32)
    if cols: v *= np.repeat(np.exp2(rng.integers(-cols, cols + 1, shape[:-2] + (1, shape[-1] // 4))) * (rng.random(shape[:-2] + (1, shape[-1] // 4)) > 0.0625), 4, axis=-1).astype(np.float32)
    return mx_ref.flush(v.astype(BF))
C = 288
STEP = [1, 2, 4]
GROUP, PLACE = np.arange(8)[:, None], np.arange(C)
def numbers_of(rng):
    return {"x": np.array(f(rng, N, 128, 4 * C)), "u": np.array(f(rng, N, 128, 512)), "v": np.array(f(rng, N, 128, 512))}
def orders(rng):
    return rng.permuted(np.tile(np.arange(C), (N, 8, 1)), axis=2)
def paired(e):
    k = np.zeros_like(e)
    np.put_along_axis(k, e[:, :, 0::2], e[:, :, 1::2], 2)
    np.put_along_axis(k, e[:, :, 1::2], e[:, :, 0::2], 2)
    return k
def stored(p, q, mu):
    return {a: np.stack([gtable(k[r]) for r in range(N)]) for a, k in (("pl", p), ("ql", q), ("ml", mu))}
def lists(rng):
    return stored(paired(orders(rng)), paired(orders(rng)), paired(orders(rng)))
def layers(rng, still=[]):
    w = np.array(f(rng, N, 128, 2048)).reshape(N, 8, 16, 4, 8, 16, 4)
    for i in still:
        w[:, :, i] = 0
        w[:, :, :, :, :, i] = 0
    return w
def weights(rng, w):
    c, s = packed(np.ascontiguousarray(w).reshape(N, 128, 2048), rng)
    return {"wc": c, "ws": s}
def setup_inputs(rng):
    return {**numbers_of(rng), **lists(rng), **weights(rng, layers(rng))}
def setup_inputs_ties(rng):
    d = numbers_of(rng)
    e = orders(rng)
    mu = paired(orders(rng))
    k = np.zeros((N, 8, C))
    for r in range(N):
        h = rng.permutation(8)
        c = rng.integers(0, C, 2)
        k[r, h[1], min(c[0], mu[r, h[1], c[0]])] = -1
        k[r, h[2], max(c[1], mu[r, h[2], c[1]])] = -1
        k[r, h[3], e[r, h[3], :2]] = -1
        k[r, h[4]] = rng.integers(-4, 0, C)
        k[r, h[5]] = rng.integers(-1, 3, C)
        k[r, h[6]] = rng.integers(1, 4, C)
        k[r, h[7]] = rng.integers(0, 2, C)
        k[r, h[7], e[r, h[7], 0]] = -1
        k[r, h[7], e[r, h[7], 2 * rng.integers(1, C // 2)]] = -1
    x = d["x"].reshape(N, 8, 16, C, 4)
    x[:, :, 0] = 0
    x[:, :, 0, :, 0] = k.astype(np.float32).astype(BF)
    u = d["u"].reshape(N, 128, 128, 4)
    u[:, :, ::16] = 0
    for h in range(0, 128, 16): u[:, h, h, 0] = 1
    return {"x": x.reshape(N, 128, 4 * C), "u": u.reshape(N, 128, 512), "v": d["v"], **stored(paired(e), paired(np.roll(e, -1, axis=2)), mu), **weights(rng, layers(rng, [0]))}
def setup_inputs_near(rng):
    d = numbers_of(rng)
    x = d["x"].astype(np.float32).reshape(N, 8, 16, C, 4)
    x[:, :, :2] = 0
    x[:, :, 8:] = 0
    x[:, :, 1, :, 0] = rng.choice([-1.0, 1.0], (N, 8, C)) * (1.0 + 0.125 * rng.integers(0, 8, (N, 8, C))) * 2.0 ** -7
    u = d["u"].reshape(N, 128, 128, 4)
    u[:, :, ::16] = 0
    w = layers(rng, [0, 1, 8, 9, 10, 11, 12, 13, 14, 15])
    o = rng.permutation(N) % 4
    for r in range(N):
        c = rng.choice([-1.0, 1.0], (8, 1))
        s = rng.integers(0, 16, (8, C))
        digits = ((s[:, :, None] >> np.arange(4)) & 1) * np.exp2(np.arange(4) - 23.0)
        if o[r] < 2:
            x[r, :, 0, :, 0] = c
            x[r, :, 8] = digits
            x[r, :, 11, :, 0] = 2.0 ** -10
        elif o[r] == 2: x[r, :, 8] = digits * rng.choice([-1.0, 1.0], (8, C, 1))
        else:
            x[r, :, 8, :, 0] = np.where(s < 8, 1.25, 0.0) * 2.0 ** -29 * c
            x[r, :, 9, :, 0] = np.where(s < 8, 0.0, 1.125) * 2.0 ** -29 * c
            x[r, :, 12, :, 0] = 2.0 ** -28
            for g in range(8): w[r, g, 1, 0, g, 10, 0] = 2.0 ** -30
            for i, g in enumerate(rng.permutation(8)[:4]):
                if i < 2:
                    e = rng.choice([-1.0, 1.0], C) * 2.0 ** -29
                    x[r, g, 8, :, 0] = 1.25 * e
                    x[r, g, 9, :, 0] = -1.125 * e
                else:
                    x[r, g, 8:] = 0
                    x[r, g, 12, :, 0] = 2.0 ** -30
                    w[r, g, 1, 0, g, 10, 0] = -2.0 ** -30
                    w[r, g, 1, 0, g, 11, 0] = 2.0 ** -30
        at = [0, C - 1, int(rng.integers(C)), int(rng.integers(C))]
        for g, j in zip(rng.permutation(8)[:4], at): x[r, g, 0, j, 0] = 2.0 ** 29 * rng.choice([-1.0, 1.0])
        k = 1.0 if o[r] == 0 else 2.0 ** -30
        for h in range(0, 128, 16):
            u[r, h, h, 0] = k if o[r] < 2 else 1.0
            if o[r] < 2: u[r, h + 11, h, 0] = k
            if o[r] < 3: u[r, h + 8, h] = k
            else:
                u[r, h + 8, h, 0] = k
                u[r, h + 9, h, 0] = 1.125 * k
                u[r, h + 10, h, 0] = k
                u[r, h + 11, h, 0] = 1.125 * k
    return {"x": x.reshape(N, 128, 4 * C).astype(BF), "u": u.reshape(N, 128, 512), "v": d["v"], **lists(rng), **weights(rng, w)}
def setup_inputs_odd(rng):
    d = numbers_of(rng)
    x = (1.0 + (2 * rng.integers(0, 64, (N, 16, 8, C, 4)) + 1) * 2.0 ** -7) * np.exp2(-rng.integers(0, 7, (N, 16, 8, C, 4)).astype(np.float64)) * rng.choice([-1.0, 1.0], (N, 16, 8, C, 4))
    x[:, :, 0, :, 0] = 1.96875 * 2.0 ** 8 * rng.choice([-1.0, 1.0], (N, 16, C))
    x[:, 1::2, 0, :, 0] *= np.where(rng.random((N, 8, C)) < 0.5, 2.0 ** -6, 1.0)
    u = d["u"].reshape(N, 16, 8, 128, 4)
    u[:, :, 0, ::16] = 0
    for r in range(N):
        for i, g in enumerate(rng.permutation(8)[:4]):
            x[r, 2 * g, 1, :, 0] = (8 + rng.integers(0, 2, C)) * 2.0 ** (i - 8)
            u[r, :, :, 16 * g] = 0
            u[r, 2 * g, 1, 16 * g, 0] = 1.0
    return {"x": x.astype(np.float32).reshape(N, 128, 4 * C).astype(BF), "u": u.reshape(N, 128, 512), "v": d["v"], **lists(rng), **weights(rng, layers(rng, [0, 8]))}
def setup_inputs_ends(rng):
    d = numbers_of(rng)
    o, e = rng.permutation(N) % 2, rng.permutation(N) % 4
    sign = rng.choice([-1.0, 1.0], (128, 1, 4))
    half = np.repeat(rng.choice([0.5, 1.0], (N, 1, C, 2)), 2, axis=3)
    small = sign * (1.0 + 0.125 * rng.integers(0, 8, (N, 128, C, 4))) * 2.0 ** -30
    x = sign * half * (14 + rng.integers(0, 3, (N, 128, C, 4))) * 2.0 ** 26
    x[o == 1] = small[o == 1]
    x[:, 112:120] = sign[112:120]
    x[:, 120:] = small[:, 120:]
    size = np.where(o == 0, 2.0 ** 30, 2.0 ** -30)
    kinds = np.array([[1, 1, 1, 1]] * 2 + [[-1, -1, -1, -1]] * 3 + [[1, 1, -1, -1]] * 2 + [[0, 0, 0, 0]])
    u = d["u"].astype(np.float32).reshape(N, 128, 128, 4)
    for r in range(N): u[r, :, ::16] = sign * kinds[rng.permutation(8)][None] * size[r]
    u[:, 112:, ::16] = 0
    v = rng.choice([-1.0, 1.0], (N, 128, 512)) * size[:, None, None]
    a = orders(rng)
    p, q, mu = paired(a), paired(np.roll(a, -1, axis=2)), paired(orders(rng))
    q[e == 1] = p[e == 1]
    mu[e == 1] = p[e == 1]
    p[e == 2] = C - 1 - np.arange(C)
    q[e == 2] = np.arange(C) ^ 1
    q[e == 3] = paired(orders(rng))[e == 3]
    w = np.zeros((N, 128, 4, 128, 4), np.float32)
    i, n = np.arange(112), np.arange(8)
    for b in range(4):
        for r in range(N):
            if o[r] == 0: w[r, i, b, i, b] = -4.0
            w[r, (120 if b < 2 else 96) + n, b, 112 + n, b] = 2.0 ** 30 if b < 2 else 2.0 ** -30
    return {"x": x.astype(np.float32).reshape(N, 128, 4 * C).astype(BF), "u": u.reshape(N, 128, 512).astype(BF), "v": v.astype(np.float32).astype(BF), **stored(p, q, mu), **weights(rng, w.astype(BF))}
def setup_inputs_spread(rng):
    d = setup_inputs(rng)
    d["x"] = wide(rng, N, 128, 4 * C, cols=6)
    return d
def check_inputs(d):
    b = []
    for k in ("x", "u", "v"):
        a = np.abs(d[k].astype(np.float32))
        if not (np.isfinite(a).all() and ((a == 0) | (a >= 2.0 ** -30) & (a <= 2.0 ** 30)).all()): b.append("a value of " + k)
    for k in ("pl", "ql", "ml"):
        for r in range(N):
            e = gentries(d[k][r])
            if not ((e >= 0) & (e < C)).all(): b.append("an entry of " + k)
            elif (e == PLACE).any() or (e[GROUP, e] != PLACE).any(): b.append(k + ": no involution without fixed points")
    none, least, most = [emit(mx_ref.quantize(np.full((128, 16), k, np.float32).astype(BF)))[1][0, 0] for k in (0.0, 2.0 ** -30, 2.0 ** 30)]
    for r in range(N):
        if ((d["wc"][r] == 0x7F) | (d["wc"][r] == 0xFF)).any(): b.append("wc: a code that is no number")
        s = mx_ref.live(d["ws"][r])
        if ((s != none) & ((s < least) | (s > most))).any(): b.append("ws: a scale out of range")
        if (((d["wc"][r].reshape(16, 8, 512, 4) & 0x7F) != 0) & (s == none)[:, None, :, None]).any(): b.append("wc: a code other than zero under the scale of zeros")
    return b
def powers(a):
    k = [np.tile(PLACE, (8, 1))]
    for i in range(C // 2 - 1): k.append(a[GROUP, k[-1]])
    return np.stack(k)
def mirror(p, q, stop):
    ahead, back = powers(q[GROUP, p]), powers(p[GROUP, q])
    i, j = np.argmax(stop[GROUP, ahead], axis=0), np.argmax(stop[GROUP, back], axis=0)
    return ahead[i, GROUP, back[j, GROUP, PLACE]]
def reference(x, u, v, pl, ql, ml, wc, ws):
    qu = [mx_ref.quantize(u[r]) for r in range(N)]
    lay = [pk(wc[r], ws[r]) for r in range(N)]
    p, q, mu = [[gentries(a[r]).astype(np.int64) for r in range(N)] for a in (pl, ql, ml)]
    now = [x[r] for r in range(N)]
    for step in STEP:
        own, sent, image = [], [], []
        for r in range(N):
            t = mx_ref.quantize(now[r])
            s = mx_ref.matmul(qu[r], t)[::16] + np.float32(0.0)
            d = decode(t).astype(BF)
            m = mirror(p[r], q[r], s < 0)
            z = (gcols(d, m).astype(np.float32) + gcols(d, q[r][GROUP, p[r]]).astype(np.float32)) * np.float32(0.5)
            sent.append(mx_ref.quantize(z.astype(BF)))
            w = (PLACE < mu[r]) & (s[GROUP, m] > s[GROUP, m[GROUP, mu[r]]])
            e = np.where(w | w[GROUP, mu[r]], mu[r], PLACE)
            q[r] = e[GROUP, q[r][GROUP, e]]
            own.append(d)
            image.append(m)
        now = [tile([gpick(mx_ref.matmul(pick(lay[r], np.arange(128 * b, 128 * b + 128)), sent[r ^ step]) * np.float32(0.03125), image[r]) + own[r][:, b::4].astype(np.float32) for b in range(4)]) for r in range(N)]
    y, qo = np.zeros((N, 128, C), np.float32), np.zeros((N, 8, C), np.float32)
    oc, osc = np.zeros((N, 128, 4 * C), np.uint8), np.zeros((N, 16, C), np.uint8)
    for r in range(N):
        t = mx_ref.quantize(now[r])
        y[r] = mx_ref.matmul(mx_ref.quantize(v[r]), t)
        qo[r] = q[r]
        oc[r], osc[r] = emit(t)
    return {"y": y, "qo": qo, "oc": oc, "osc": osc}

@@ -1,0 +1,415 @@
+from concourse.bass import DstId, RemoteDMATransfer
+from concourse.mybir import dt, AluOpType as O, ActivationFunctionType as AF
+
+C = 288
+K = C // 16
+STEPS = [1, 2, 4]
+JUMPS = [(0, 1), (1, 2), (2, 4), (3, 8), (4, 16), (4, 16), (5, 32), (6, 64)]
+SEEN = 143
+CUT = 18
+TINY, PLAIN, HALF, GATHER, SCATTER, NEAR, WAKE, BIAS, LOOK, SLACK, FLIGHT = 0.082, 0.31, 0.232, 0.488, 2.082, 0.064, 0.191, 0.555, 0.402, 0.094, 5.5
+MID = 144
+UNIT, LIFT = 512, 8
+HOLD, DROP = float(2 ** 19), float(-2 ** 21)
+GAIN = float(2 ** 20)
+
+F32, BF, F16, I32, U16, U8, MX = "float32", "bfloat16", "float16", "int32", "uint16", "uint8", "float8_e4m3fn_x4"
+
+
+def sb(n, d):
+    return ("sbuf", [128, n], d)
+
+
+SCRATCH = {
+    "xt": sb(4 * C, BF), "ut": sb(512, BF), "vt": sb(512, BF),
+    "pi": sb(K, I32), "qi": sb(K, I32), "mi": sb(K, I32),
+    "wq": sb(512, MX), "wp": sb(512, U8), "uq": sb(128, MX), "up": sb(128, U8), "ur": sb(128, MX), "urp": sb(128, U8),
+    "vq": sb(128, MX), "vp": sb(128, U8), "eq": sb(512, MX), "ep": sb(512, U8),
+    "tq": sb(C, MX), "tp": sb(C, U8), "zq": sb(C, MX), "zp": sb(C, U8),
+    "et": sb(2048, BF), "one": sb(512, BF), "zt": sb(4 * C, BF),
+    "cc": sb(2 * C, BF), "tm": sb(C, F32), "dif": sb(C, F32), "ka": sb(C, F32), "kb": sb(C, F32),
+    "hc": sb(C, F32), "hh": sb(2 * C, F16), "hm": sb(2 * C, F16), "ones": sb(2 * C, BF),
+    "pp": sb(1, I32), "pm": sb(1, I32), "pf": sb(1, F32), "cor": sb(1, F32), "coj": sb(1, F32), "coh": sb(1, F32),
+    "cw0": sb(K, F32), "cw": sb(K, F32), "ou0": sb(8, I32), "ou": sb(8, U16),
+    "w0": sb(C, F32), "wm0": sb(C, F32), "cd": sb(C, F32),
+    "pw": sb(K, U16), "qw": sb(K, U16), "low": sb(K, U16), "hiw": sb(K, U16), "dmw": sb(K, F32), "muf": sb(K, F32),
+    "qa": sb(C, BF), "qb": sb(C, BF), "ex": sb(C, F32), "eh": sb(2 * C, F16),
+    "wa": sb(C, F32), "wb": sb(C, F32), "wm": sb(C, F32),
+    "dd": sb(C, F32), "ctr": sb(C, F32), "c5": sb(C, F32), "buf": sb(C + 8, F32), "bg": sb(C, F32), "lg": sb(C, BF),
+    "vi": sb(K, I32), "lw": sb(K, U16), "tw": sb(K, I32), "t2": sb(K, F32), "ll": sb(K, F32),
+    "ps2": sb(2 * K, F32), "pos": sb(2 * K, U16), "posr": sb(K, U16), "lin": sb(2 * C, BF), "linw": sb(2 * K, U16),
+    "nf": sb(C, BF), "ss": sb(C, F32), "g2": sb(2 * C, BF), "fs": sb(2 * C, BF), "rs": sb(2 * C, BF), "ij": sb(2 * C, BF), "eij": sb(2 * C, F16),
+    "cq": sb(K, F32), "lc": sb(2 * K, F32), "k3": sb(2 * K, F32), "de": sb(K, F32), "zl": sb(K, F32), "zm": sb(K, F32), "dp": sb(K, F32), "of": sb(K, F32), "ow": sb(K, U16),
+    "mf": sb(C, BF), "mw": sb(K, U16),
+    "st": sb(C, F32), "su": sb(C, F32), "sg": sb(C, BF),
+    "sw": sb(K, U16), "sf": sb(C, BF), "yf": sb(C, BF), "yw": sb(K, U16),
+    "hb": sb(4 * C, BF), "ga": sb(4 * C, BF), "rb": sb(4 * C, F32), "mb": sb(4 * C, F32), "yo": sb(C, F32),
+    "ps": ("psum", [128, 4096], F32),
+}
+for _k in range(3):
+    SCRATCH["rq%d" % _k] = sb(C, MX)
+    SCRATCH["rp%d" % _k] = sb(C, U8)
+for _k in range(7):
+    SCRATCH["xf%d" % _k] = sb(C, BF)
+    SCRATCH["xw%d" % _k] = sb(K, U16)
+LOADS = ["pi", "qi", "mi", "xt", "ut", "vt", "wq", "wp"]
+STORES = ["oy", "oq", "occ", "oss"]
+SEMAPHORES = ["v", "s", "t", "g"] + ["ld_" + a for a in LOADS] + ["st_" + a for a in STORES] + ["arr%d" % k for k in range(3)] + ["snt%d" % k for k in range(3)]
+
+
+def rank_program(g, core, T, topo):
+    rank = T.rank_of(core)
+    if rank is None:
+        return
+    queue = {"v": g.vector, "s": g.scalar, "t": g.tensor, "g": g, "y": g.sync}
+    count, known, snap = {}, {e: {} for e in queue}, {}
+    last, readers = {}, {}
+
+    def settle(e, tokens):
+        for s, n in sorted(tokens, key=lambda a: (a[0] == e, -a[1])):
+            if known[e].get(s, 0) >= n: continue
+            queue[e].wait_ge(T.sem[s], n)
+            for a, b in list(snap.get((s, n), {}).items()) + [(s, n)]:
+                known[e][a] = max(known[e].get(a, 0), b)
+
+    def issue(n, e):
+        tokens = set()
+        for k in n["rd"]:
+            if k in last: tokens.add(last[k])
+        for k in n["wr"]:
+            if k in last: tokens.add(last[k])
+            tokens |= readers.get(k, set())
+        settle(e, tokens)
+        s = n["sem"] or e
+        n["make"][e]().then_inc(T.sem[s], n["inc"])
+        count[s] = count.get(s, 0) + n["inc"]
+        token = (s, count[s])
+        snap[token] = dict(known[e])
+        snap[token][s] = count[s]
+        for k in n["wr"]: last[k], readers[k] = token, set()
+        for k in n["rd"]: readers.setdefault(k, set()).add(token)
+
+    nodes = []
+
+    def op(e, make, rd, wr, sem=None, inc=1, cost=TINY, lat=0.0, other=None, send=None):
+        nodes.append(dict(make={e: make} if other is None else {e: make, other[0]: other[1]}, rd=rd, wr=wr, sem=sem, inc=inc, cost=cost, lat=lat, send=send))
+
+    V, S = g.vector, g.scalar
+
+    def ts(out, in0, s1, s2, o0, o1, rd, wr, cost=TINY):
+        if o1 is None: op("v", lambda: V.tensor_scalar(out, in0, s1, None, o0), rd, wr, cost=cost)
+        else: op("v", lambda: V.tensor_scalar(out, in0, s1, s2, o0, o1), rd, wr, cost=cost)
+
+    def tt(out, a, b, o, rd, wr, cost=TINY):
+        op("v", lambda: V.tensor_tensor(out, a, b, o), rd, wr, cost=cost)
+
+    def cp(out, a, rd, wr, cost=TINY):
+        op("v", lambda: V.tensor_copy(out, a), rd, wr, cost=cost)
+
+    def either(out, a, rd, wr, cost=GATHER):
+        op("s", lambda: S.activation(out, a, AF.Copy), rd, wr, cost=cost, other=("v", lambda: V.tensor_copy(out, a)))
+
+    def act(out, a, f, rd, wr, bias=0.0, scale=1.0, cost=GATHER):
+        if bias == 0.0 and scale == 1.0: op("s", lambda: S.activation(out, a, f), rd, wr, cost=cost)
+        else: op("s", lambda: S.activation(out, a, f, bias=bias, scale=scale), rd, wr, cost=PLAIN)
+
+    def scan(out, a, b, init, o0, o1, rd, wr, cost=PLAIN):
+        op("v", lambda: V.tensor_tensor_scan(out, a, b, init, o0, o1), rd, wr, cost=cost)
+
+    def load(e, name, out, in_):
+        op(e, lambda: queue[e].dma_start(out, in_), [], [name], "ld_" + name, 16, cost=0.1, lat=2.5)
+
+    def ordered():
+        wrote, read, preds, succ = {}, {}, [], []
+        for i, n in enumerate(nodes):
+            p = set()
+            for k in n["rd"]:
+                if k in wrote: p.add(wrote[k])
+            for k in n["wr"]:
+                if k in wrote: p.add(wrote[k])
+                p |= read.get(k, set())
+            for k in n["wr"]: wrote[k], read[k] = i, set()
+            for k in n["rd"]: read.setdefault(k, set()).add(i)
+            p.discard(i)
+            preds.append(p)
+            succ.append([])
+            for j in p: succ[j].append(i)
+        rank_ = [0.0] * len(nodes)
+        for i in range(len(nodes) - 1, -1, -1):
+            rank_[i] = nodes[i]["cost"] + nodes[i]["lat"] + max([rank_[j] + WAKE for j in succ[i]] + [0.0])
+        free, at, end, todo = {e: 0.0 for e in queue}, {}, {}, [len(p) for p in preds]
+        open_, out = [i for i in range(len(nodes)) if not preds[i]], []
+        while open_:
+            best, spots = {}, {}
+            waiting = min([max([end[j] + (NEAR if at[j] == "v" else WAKE) for j in preds[i]] + [0.0]) for i in open_ if list(nodes[i]["make"]) == ["v"]] + [1e9])
+            for i in open_:
+                spot = None
+                for e in nodes[i]["make"]:
+                    r = max([end[j] + (NEAR if at[j] == e else WAKE) for j in preds[i]] + [0.0])
+                    t = max(r, free[e])
+                    a = (t + (BIAS if e == "v" and len(nodes[i]["make"]) > 1 and waiting < t + GATHER * LOOK else 0.0), e, r)
+                    if spot is None or a < spot: spot = a
+                spots[i] = spot
+                e, r = spot[1], max(spot[2], free[spot[1]])
+                best[e] = min(best.get(e, 1e9), r)
+            e = min(best, key=lambda a: (best[a], a))
+            i = max([j for j in open_ if spots[j][1] == e and max(spots[j][2], free[e]) <= best[e] + SLACK], key=lambda j: (rank_[j], -j))
+            t = max(spots[i][2], free[e])
+            free[e], at[i], end[i] = t + nodes[i]["cost"], e, t + nodes[i]["cost"] + nodes[i]["lat"]
+            open_.remove(i)
+            out.append((nodes[i], e))
+            for j in succ[i]:
+                todo[j] -= 1
+                if not todo[j]: open_.append(j)
+        return out
+
+    def held(name):
+        scan(T.ex[:], T.hc[:], T[name][:], 0.0, O.add, O.max, ["hc", name], ["ex"])
+        return T.ex[:, 15:C:16]
+
+    def unwrap(name, n, w, more=[]):
+        scan(T.eh[:, 0:n], T.hh[:, 0:n], T[name][:, 0:n], 0.0, O.add, O.max, ["hh", name] + more, ["eh"], HALF * n / C)
+        ts(T[w][:, 0:n // 16], T.eh[:, 15:n:16], T.coh[:, 0:1], None, O.subtract, None, ["eh", "coh"], [w])
+
+    def bank(b, n=C):
+        return T.ps[:, 512 * b:512 * b + n]
+
+    def mm(b, l, ls, a, r, rs, key=None):
+        op("t", lambda: g.tensor.matmul_mx(bank(b), T[l][:, a:a + 128], T[ls][:, a:a + 128], T[r][:, 0:C], T[rs][:, 0:C], True, True),
+           [r, rs] + ([key] if key else [l, ls]), ["ps%d" % b], cost=0.3)
+
+    def quant(q, p, t, n, rd=None):
+        op("v", lambda: V.quantize_mx(T[q][:, 0:n], T[p][:, 0:n], T[t][:, 0:4 * n]), rd or [t], [q, p], cost=0.32)
+
+    def iota(name, out, pattern, base, mul, small=True):
+        cost = 0.14 + 0.002 * (C if len(pattern) > 1 else pattern[0][1])
+        if small: op("g", lambda: g.iota(out, pattern, base, mul, allow_small_or_imprecise_dtypes=True), [], [name], cost=cost)
+        else: op("g", lambda: g.iota(out, pattern, base, mul), [], [name], cost=cost)
+
+    load("y", "pi", T.pi[:], T.pl[:])
+    load("s", "qi", T.qi[:], T.ql[:])
+    load("y", "xt", T.xt[:], T.x[:])
+    load("y", "ut", T.ut[:], T.u[:])
+    load("y", "mi", T.mi[:], T.ml[:])
+    load("y", "wq", T.wq[:].bitcast(dt.uint8), T.wc[:])
+    load("y", "wp", T.wp[:], T.ws[:])
+    load("y", "vt", T.vt[:], T.v[:])
+
+    iota("pp", T.pp[:], [[1, 1]], 0, 1, False)
+    iota("tm", T.tm[:], [[0, K], [1, 16]], 0, 0)
+    iota("cc", T.cc[:, 0:C], [[1, C]], -MID, 0)
+    iota("wm0", T.wm0[:], [[UNIT, C]], LIFT + SEEN - 1, 0)
+    iota("w0", T.w0[:], [[UNIT, C]], LIFT + SEEN, 0)
+    iota("ou0", T.ou0[:], [[16, 8]], 0, 0, False)
+    iota("cw0", T.cw0[:], [[16, K]], 0, 0)
+    op("v", lambda: V.memset(T.one[:], 1.0), [], ["one"])
+    for b in range(4):
+        op("g", lambda b=b: g.affine_select(T.et[:, 512 * b:512 * b + 512], T.one[:], [[-1, 512]], O.is_equal, 0.0, b, 4), ["one"], ["et%d" % b], cost=1.2)
+    iota("cd", T.cd[:], [[UNIT, C]], LIFT - 1, 0)
+    ts(T.pm[:], T.pp[:], 15, None, O.bitwise_and, None, ["pp"], ["pm"])
+    cp(T.pf[:], T.pm[:], ["pm"], ["pf"])
+    ts(T.cor[:], T.pf[:], 15.0, HOLD, O.is_lt, O.mult, ["pf"], ["cor"])
+    ts(T.dif[:], T.tm[:], T.pf[:, 0:1], None, O.subtract, None, ["tm", "pf"], ["dif"])
+    ts(T.ka[:], T.dif[:], 0.0, DROP, O.is_equal, O.mult, ["dif"], ["ka"])
+    ts(T.kb[:], T.dif[:], 1.0, HOLD, O.is_equal, O.mult, ["dif"], ["kb"])
+    tt(T.hc[:], T.ka[:], T.kb[:], O.add, ["ka", "kb"], ["hc"])
+    ts(T.hh[:, 0:C], T.hc[:], 2.0 ** -10, None, O.mult, None, ["hc"], ["hh"])
+    ts(T.coh[:], T.cor[:], 2.0 ** -10, float(MID), O.mult, O.subtract, ["cor"], ["coh"])
+
+    cp(T.qw[:], T.qi[:], ["qi"], ["qw"])
+    cp(T.pw[:], T.pi[:], ["pi"], ["pw"])
+    act(T.qa[:], T.cc[:, 0:C].indirect(T.qw[:]), AF.Copy, ["cc", "qw"], ["qa"])
+    act(T.xf0[:], T.qa[:].indirect(T.pw[:]), AF.Copy, ["qa", "pw"], ["xf0"])
+    op("v", lambda: V.memset(T.ones[:], 1.0), [], ["ones"], cost=PLAIN)
+    op("v", lambda: V.memset(T.buf[:, 0:8], 0.0), [], ["buf"])
+    cp(T.cc[:, C:2 * C], T.cc[:, 0:C], ["cc"], ["cd2"], HALF)
+    cp(T.hh[:, C:2 * C], T.hh[:, 0:C], ["hh"], ["hh2"], HALF)
+    cp(T.ou[:], T.ou0[:], ["ou0"], ["ou"])
+
+    def jump():
+        unwrap("xf0", C, "xw0")
+        w, wm, made = "w0", "wm0", 0
+        for n, (k, s) in enumerate(JUMPS):
+            if n:
+                act(T.wm[:], T[w][:], AF.Identity, [w], ["wm"], bias=-float(s))
+                wm = "wm"
+            nxt = "wb" if w == "wa" else "wa"
+            tt(T[nxt][:], T[w][:].indirect(T["xw%d" % k][:]), T[wm][:], O.min, [w, "xw%d" % k, wm], [nxt], GATHER)
+            w = nxt
+            if made == k and k < 6:
+                either(T["xf%d" % (k + 1)][:], T["xf%d" % k][:].indirect(T["xw%d" % k][:]), ["xf%d" % k, "xw%d" % k], ["xf%d" % (k + 1)])
+                unwrap("xf%d" % (k + 1), C, "xw%d" % (k + 1))
+                made = k + 1
+        tt(T.dd[:], T[w][:].indirect(T.xw0[:]), T.cd[:], O.subtract, [w, "xw0", "cd"], ["dd"], GATHER)
+        for a, c in (("c5", 2.0), ("ctr", 1.0)):
+            op("s", lambda a=a, c=c: S.activation(T[a][:], T.dd[:], AF.Relu, scale=c), ["dd"], [a], cost=PLAIN,
+               other=("v", lambda a=a, c=c: V.tensor_scalar(T[a][:], T.dd[:], 0.0, c, O.max, O.mult)))
+        a = held(w)
+        ts(T.lw[:], a, T.cor[:, 0:1], 1.0 / UNIT, O.subtract, O.mult, ["ex", "cor"], ["lw"])
+        ts(T.vi[:], a, T.cor[:, 0:1], float(LIFT), O.subtract, O.subtract, ["ex", "cor"], ["vi"])
+        scan(T.buf[:, 1:C + 1], T.ones[:, 0:C], T.c5[:], 0.0, O.mult, O.add, ["ones", "c5"], ["buf"])
+        either(T.bg[:], T.buf[:, 0:C].indirect(T.lw[:]), ["buf", "lw"], ["bg"])
+        ts(T.tw[:], T.vi[:], UNIT - 1, None, O.bitwise_and, None, ["vi"], ["tw"])
+        ts(T.t2[:], T.tw[:], T.cor[:, 0:1], None, O.subtract, None, ["tw", "cor"], ["t2"])
+        either(T.lg[:], T.ctr[:].indirect(T.lw[:]), ["ctr", "lw"], ["lg"])
+        scan(T.eh[:, 0:C], T.hh[:, 0:C], T.lg[:], 0.0, O.add, O.max, ["hh", "lg"], ["eh"], HALF)
+        ts(T.ll[:], T.eh[:, 15:C:16], T.coh[:, 0:1], float(MID), O.subtract, O.subtract, ["eh", "coh"], ["ll"])
+        a = held("bg")
+        tt(T.ps2[:, 0:K], a, T.t2[:], O.add, ["ex", "t2"], ["psa"])
+        tt(T.ps2[:, K:2 * K], T.ps2[:, 0:K], T.ll[:, 0:K], O.add, ["psa", "ll"], ["psb"])
+        cp(T.pos[:], T.ps2[:], ["psa", "psb"], ["pos"])
+        cp(T.lin[:].indirect(T.pos[:]), T.cc[:], ["pos", "cc", "cd2"], ["lin"], SCATTER)
+        for a, w in ((0, "lca"), (K, "lcb")): ts(T.lc[:, a:a + K], T.ll[:], T.coj[:, 0:1], None, O.add, None, ["ll", "coj"], [w])
+        ts(T.posr[:], T.ps2[:, 0:K], -1.0, float(2 * C - 1), O.mult, O.add, ["psa"], ["posr"])
+        unwrap("lin", 2 * C, "linw", ["hh2"])
+
+    def products():
+        mm(4, "ur", "urp", 0, "tq", "tp")
+        for b in range(4): mm(b, "eq", "ep", 128 * b, "tq", "tp", "eq%d" % b)
+
+    def times(out, a, c, rd, wr):
+        op("s", lambda: S.activation(out, a, AF.Identity, scale=c), rd, wr, cost=PLAIN, other=("v", lambda: V.tensor_scalar(out, a, c, None, O.mult)))
+
+    def halves():
+        for b in range(4): times(T.hb[:, C * b:C * b + C], bank(b), 0.5, [], ["ps%d" % b, "hb%d" % b])
+
+    def aside():
+        for b in range(4):
+            either(T.ga[:, b:4 * C:4], T.hb[:, C * b:C * b + C].indirect(T.xw0[:]), ["hb%d" % b, "xw0"], ["ga%d" % b])
+
+    def prepare():
+        ts(T.hm[:], T.hh[:], 2.0, None, O.mult, None, ["hh", "hh2"], ["hm"], PLAIN)
+        ts(T.coj[:], T.cor[:], 2.0 ** -9, None, O.mult, None, ["cor"], ["coj"])
+
+    def prepare2():
+        ts(T.cw[:], T.cw0[:], T.pf[:, 0:1], None, O.add, None, ["cw0", "pf"], ["cw"])
+        tt(T.dmw[:], T.mi[:], T.cw[:], O.subtract, ["mi", "cw"], ["dmw"])
+        ts(T.muf[:], T.dmw[:], T.cor[:, 0:1], 2.0 ** -10, O.mult, O.mult, ["dmw", "cor"], ["muf"])
+        tt(T.cq[:], T.cw[:], T.muf[:], O.subtract, ["cw", "muf"], ["cq"])
+        for w, o in (("low", O.min), ("hiw", O.max)):
+            tt(T.muf[:], T.mi[:], T.cw[:], o, ["mi", "cw"], ["muf"])
+            cp(T[w][:], T.muf[:], ["muf"], [w])
+
+    def first():
+        quant("uq", "up", "ut", 128)
+        cp(T.ur[:].bitcast(dt.uint32), T.uq[:].bitcast(dt.uint32).indirect(T.ou[:]), ["uq", "ou"], ["ur"])
+        cp(T.urp[:], T.up[:].indirect(T.ou[:]), ["up", "ou"], ["urp"])
+        quant("tq", "tp", "xt", C)
+
+    def constants():
+        for b in range(4):
+            op("v", lambda b=b: V.quantize_mx(T.eq[:, 128 * b:128 * b + 128], T.ep[:, 128 * b:128 * b + 128], T.et[:, 512 * b:512 * b + 512]), ["et%d" % b], ["eq%d" % b], cost=0.15)
+        products()
+
+    first()
+    constants()
+    prepare()
+    prepare2()
+    jump()
+    quant("vq", "vp", "vt", 128)
+
+    qcur = ["qa", "qb"]
+    for k, step in enumerate(STEPS):
+        final = k == 2
+        peer = T.cores[rank ^ step]
+        rid, pid = topo.addr(peer, core)
+        mask = topo.mask(core, peer)
+        width = len(topo.engines(core, peer))
+        ts(T.nf[:], bank(4), 0.0, None, O.is_ge, None, [], ["ps4", "nf"], PLAIN)
+        cp(T.g2[:, 0:16 * CUT], T.nf[:].indirect(T.linw[:, 0:CUT]), ["nf", "linw"], ["g2a"], GATHER * CUT / K)
+        act(T.g2[:, 16 * CUT:2 * C], T.nf[:].indirect(T.linw[:, CUT:2 * K]), AF.Copy, ["nf", "linw"], ["g2b"], cost=GATHER * (2 * K - CUT) / K)
+        act(T.ss[:], bank(4), AF.Copy, [], ["ps4", "ss"], cost=PLAIN)
+        scan(T.fs[:], T.g2[:], T.ones[:], 1.0, O.mult, O.add, ["g2a", "g2b", "ones"], ["fs"])
+        act(T.ij[:, 0:C], T.fs[:].indirect(T.pos[:, K:2 * K]), AF.Copy, ["fs", "pos"], ["ija"])
+        scan(T.rs[:], T.g2[:, ::-1], T.ones[:], 1.0, O.mult, O.add, ["g2a", "g2b", "ones"], ["rs"])
+        cp(T.ij[:, C:2 * C], T.rs[:].indirect(T.posr[:]), ["rs", "posr"], ["ijb"], GATHER)
+        halves()
+        aside()
+        scan(T.eij[:], T.hm[:], T.ij[:], 0.0, O.add, O.max, ["hm", "ija", "ijb"], ["eij"])
+        tt(T.k3[:], T.eij[:, 15:2 * C:16], T.lc[:], O.min, ["eij", "lca", "lcb"], ["k3"])
+        tt(T.de[:], T.k3[:, K:2 * K], T.k3[:, 0:K], O.subtract, ["k3"], ["de"])
+        ts(T.zl[:], T.de[:], 0.0, None, O.is_lt, None, ["de"], ["zl"])
+        tt(T.dp[:], T.de[:], T.ps2[:, 0:K], O.add, ["de", "psa"], ["dp"])
+        tt(T.zm[:], T.zl[:], T.ll[:, 0:K], O.mult, ["zl", "ll"], ["zm"])
+        tt(T.of[:], T.zm[:], T.dp[:], O.add, ["zm", "dp"], ["of"])
+        cp(T.ow[:], T.of[:], ["of"], ["ow"])
+        either(T.mf[:], T.lin[:].indirect(T.ow[:]), ["lin", "ow"], ["mf"])
+        unwrap("mf", C, "mw")
+        act(T.st[:], T.ss[:].indirect(T.mw[:]), AF.Copy, ["ss", "mw"], ["st"])
+        act(T.su[:], T.st[:].indirect(T.low[:]), AF.Copy, ["st", "low"], ["su"])
+        parts = [(0, 8), (8, K)] if final else [(0, K)]
+        for h, (a, z) in enumerate(parts):
+            own = [h] if final else [0, 1]
+            zs = ["zt%d%d" % (j, b) for b in range(4) for j in own]
+            for b in range(4):
+                tt(T.zt[:, 64 * a + b:64 * z:4], T.hb[:, C * b:C * b + C].indirect(T.mw[:, a:z]), T.ga[:, 64 * a + b:64 * z:4], O.add, ["hb%d" % b, "mw", "ga%d" % b], ["zt%d%d" % (j, b) for j in own], GATHER * (z - a) / K)
+            op("v", lambda a=a, z=z: V.quantize_mx(T.zq[:, 16 * a:16 * z], T.zp[:, 16 * a:16 * z], T.zt[:, 64 * a:64 * z]), zs, ["zq0", "zq1"][h:], cost=0.32 * (z - a) / K)
+
+            def send(k=k, pid=pid, rid=rid, mask=mask, a=16 * a, z=16 * z, h=h, n=2 * width * len(parts)):
+                settle("g", {last["zq%d" % h]})
+                land, sent = T.sem["arr%d" % k], T.sem["snt%d" % k]
+                g.remote_dma(T["rq%d" % k][:, a:z].bitcast(dt.uint8), T.zq[:, a:z].bitcast(dt.uint8), land, sent, pid, rid, mask)
+                g.remote_dma(T["rp%d" % k][:, a:z], T.zp[:, a:z], land, sent, pid, rid, mask)
+                readers.setdefault("zq%d" % h, set()).add(("snt%d" % k, n))
+                for r in ("rq%d" % k, "rp%d" % k): last[r] = ("arr%d" % k, n)
+                count["arr%d" % k] = count["snt%d" % k] = n
+
+            op("g", None, ["zq%d" % h], ["rq%d" % k, "rp%d" % k], cost=0.6, lat=FLIGHT, send=send)
+        tt(T.sg[:], T.st[:].indirect(T.hiw[:]), T.su[:], O.is_lt, ["st", "hiw", "su"], ["sg"], GATHER)
+        scan(T.eh[:, 0:C], T.hh[:, 0:C], T.sg[:], 0.0, O.add, O.max, ["hh", "sg"], ["eh"], HALF)
+        tt(T.zm[:], T.eh[:, 15:C:16], T.dmw[:], O.mult, ["eh", "dmw"], ["zm"])
+        tt(T.of[:], T.zm[:], T.cq[:], O.add, ["zm", "cq"], ["of"])
+        cp(T.sw[:], T.of[:], ["of"], ["sw"])
+        qo, qn = qcur[k % 2], qcur[1 - k % 2]
+        either(T.yf[:], T[qo][:].indirect(T.sw[:]), [qo, "sw"], ["yf"])
+        either(T.sf[:], T.cc[:, 0:C].indirect(T.sw[:]), ["cc", "sw"], ["sf"])
+        unwrap("yf", C, "yw")
+        either(T[qn][:], T.sf[:].indirect(T.yw[:]), ["sf", "yw"], [qn])
+        if not final:
+            either(T.xf0[:], T[qn][:].indirect(T.pw[:]), [qn, "pw"], ["xf0"])
+        else:
+            ts(T.dd[:], T[qn][:], float(MID), None, O.add, None, [qn], ["dd"], PLAIN)
+            op("y", lambda: g.sync.dma_start(T.qo[:], T.dd[0:128:16, :]), ["dd"], [], "st_oq", 16, lat=2.5)
+
+        def layer():
+            for b in range(4): mm((5, 6, 7, 4)[b], "wq", "wp", 128 * b, "rq%d" % k, "rp%d" % k)
+
+        def scaled(bs):
+            for b in bs:
+                times(T.rb[:, C * b:C * b + C], bank((5, 6, 7, 4)[b]), 0.03125, [], ["ps%d" % (5, 6, 7, 4)[b], "rb%d" % b])
+
+        def picked(bs):
+            for b in bs:
+                either(T.mb[:, C * b:C * b + C], T.rb[:, C * b:C * b + C].indirect(T.mw[:]), ["rb%d" % b, "mw"], ["mb%d" % b])
+
+        def added(bs=range(4)):
+            for b in bs:
+                tt(T.xt[:, b:4 * C:4], T.mb[:, C * b:C * b + C], bank(b), O.add, ["mb%d" % b], ["ps%d" % b, "xt%d" % b], PLAIN)
+            quant("tq", "tp", "xt", C, ["xt", "xt0", "xt1", "xt2", "xt3"])
+
+        if not final:
+            layer()
+            scaled(range(4))
+            picked(range(4))
+            added()
+            products()
+            jump()
+        else:
+            layer()
+            for b in (0, 1):
+                cp(T.mb[:, C * b:C * b + C], bank(b), [], ["ps%d" % b, "mb%d" % b], PLAIN)
+            scaled(range(4))
+            picked([2, 3])
+            for b in (0, 1):
+                tt(T.xt[:, b:4 * C:4], T.rb[:, C * b:C * b + C].indirect(T.mw[:]), T.mb[:, C * b:C * b + C], O.add, ["rb%d" % b, "mw", "mb%d" % b], ["xt%d" % b], GATHER)
+            added([2, 3])
+            op("y", lambda: g.sync.dma_start(T.oc[:], T.tq[:].bitcast(dt.uint8)), ["tq"], [], "st_occ", 16, lat=2.5)
+            for a in range(4):
+                op("y", lambda a=a: g.sync.dma_start(T.osc[4 * a:4 * a + 4, :], T.tp[32 * a:32 * a + 4, :]), ["tp"], [], "st_oss", 16, lat=2.5)
+            mm(4, "vq", "vp", 0, "tq", "tp")
+            act(T.yo[:], bank(4), AF.Copy, [], ["ps4", "yo"], cost=PLAIN)
+            op("y", lambda: g.sync.dma_start(T.y[:], T.yo[:]), ["yo"], [], "st_oy", 16, lat=2.5)
+    for n, e in ordered():
+        if n["send"]: n["send"]()
+        else: issue(n, e)
+    settle("g", set(count.items()))

@@ -1,17 +1,16 @@
-from concourse.bass import DstId, RemoteDMATransfer
 from concourse.mybir import dt, AluOpType as O, ActivationFunctionType as AF
 
 C = 288
 K = C // 16
 STEPS = [1, 2, 4]
-JUMPS = [(0, 1), (1, 2), (2, 4), (3, 8), (4, 16), (4, 16), (5, 32), (6, 64)]
-SEEN = 143
-CUT = 18
-TINY, PLAIN, HALF, GATHER, SCATTER, NEAR, WAKE, BIAS, LOOK, SLACK, FLIGHT = 0.082, 0.31, 0.232, 0.488, 2.082, 0.064, 0.191, 0.555, 0.402, 0.094, 5.5
+RADIX = [3, 3, 4, 4]
+UNIT = 146
+LEN = 145
+TOP = UNIT * C
+TINY, PLAIN, HALF, BOTH, GATHER, SCATTER, NEAR, WAKE, SLACK, FLIGHT, HOP = 0.082, 0.31, 0.2, 0.6, 0.488, 1.04, 0.064, 0.191, 0.094, 5.5, 2.5
 MID = 144
-UNIT, LIFT = 512, 8
 HOLD, DROP = float(2 ** 19), float(-2 ** 21)
-GAIN = float(2 ** 20)
+FUSED, TURNED = (0, 1), (2, 3)
 
 F32, BF, F16, I32, U16, U8, MX = "float32", "bfloat16", "float16", "int32", "uint16", "uint8", "float8_e4m3fn_x4"
 
@@ -26,35 +25,33 @@ SCRATCH = {
     "wq": sb(512, MX), "wp": sb(512, U8), "uq": sb(128, MX), "up": sb(128, U8), "ur": sb(128, MX), "urp": sb(128, U8),
     "vq": sb(128, MX), "vp": sb(128, U8), "eq": sb(512, MX), "ep": sb(512, U8),
     "tq": sb(C, MX), "tp": sb(C, U8), "zq": sb(C, MX), "zp": sb(C, U8),
-    "et": sb(2048, BF), "one": sb(512, BF), "zt": sb(4 * C, BF),
-    "cc": sb(2 * C, BF), "tm": sb(C, F32), "dif": sb(C, F32), "ka": sb(C, F32), "kb": sb(C, F32),
-    "hc": sb(C, F32), "hh": sb(2 * C, F16), "hm": sb(2 * C, F16), "ones": sb(2 * C, BF),
-    "pp": sb(1, I32), "pm": sb(1, I32), "pf": sb(1, F32), "cor": sb(1, F32), "coj": sb(1, F32), "coh": sb(1, F32),
-    "cw0": sb(K, F32), "cw": sb(K, F32), "ou0": sb(8, I32), "ou": sb(8, U16),
-    "w0": sb(C, F32), "wm0": sb(C, F32), "cd": sb(C, F32),
-    "pw": sb(K, U16), "qw": sb(K, U16), "low": sb(K, U16), "hiw": sb(K, U16), "dmw": sb(K, F32), "muf": sb(K, F32),
-    "qa": sb(C, BF), "qb": sb(C, BF), "ex": sb(C, F32), "eh": sb(2 * C, F16),
-    "wa": sb(C, F32), "wb": sb(C, F32), "wm": sb(C, F32),
-    "dd": sb(C, F32), "ctr": sb(C, F32), "c5": sb(C, F32), "buf": sb(C + 8, F32), "bg": sb(C, F32), "lg": sb(C, BF),
-    "vi": sb(K, I32), "lw": sb(K, U16), "tw": sb(K, I32), "t2": sb(K, F32), "ll": sb(K, F32),
-    "ps2": sb(2 * K, F32), "pos": sb(2 * K, U16), "posr": sb(K, U16), "lin": sb(2 * C, BF), "linw": sb(2 * K, U16),
-    "nf": sb(C, BF), "ss": sb(C, F32), "g2": sb(2 * C, BF), "fs": sb(2 * C, BF), "rs": sb(2 * C, BF), "ij": sb(2 * C, BF), "eij": sb(2 * C, F16),
-    "cq": sb(K, F32), "lc": sb(2 * K, F32), "k3": sb(2 * K, F32), "de": sb(K, F32), "zl": sb(K, F32), "zm": sb(K, F32), "dp": sb(K, F32), "of": sb(K, F32), "ow": sb(K, U16),
+    "et": sb(516, BF), "one": sb(516, BF), "zt": sb(4 * C, BF),
+    "di": sb(K, I32), "dm": sb(K, I32), "ka": sb(K, F32), "kb": sb(K, F32), "kc": sb(16, F32), "kd": sb(16, F32), "iw": sb(K, U16), "cu": sb(K, F32),
+    "cf": sb(C, F32), "ku": sb(C, F32), "kr": sb(C, F32), "hc": sb(C, F32), "hh": sb(C, BF), "cn1": sb(1, F32),
+    "pp": sb(1, I32), "pm": sb(1, I32), "pf": sb(1, F32), "cor": sb(1, F32), "coh": sb(1, F32), "con": sb(1, F32), "cn0": sb(1, F32),
+    "c72": sb(1, F32), "c73": sb(1, F32), "cln": sb(1, F32), "co2": sb(1, F32), "cov": sb(1, F32), "ctp": sb(1, F32),
+    "cw0": sb(K, F32), "cw": sb(K, F32), "kst": sb(K, F32), "kx": sb(K, F32), "kx2": sb(K, F32), "ou0": sb(8, I32), "ou": sb(8, U16),
+    "pw": sb(K, U16), "qw": sb(K, U16), "low": sb(K, U16), "hiw": sb(K, U16), "dmw": sb(K, F32), "muf": sb(K, F32), "cq": sb(K, F32),
+    "qa": sb(C, F32), "qb": sb(C, F32), "arl": sb(C, F32), "aab": sb(C, F32), "aw": sb(K, U16),
+    "ex": sb(C, F32), "ex1": sb(C, F32), "exa": sb(C, F32), "eh": sb(C, F16),
+    "nf": sb(C, BF), "ss": sb(C, F32), "v0": sb(C, F32), "v1": sb(C, F32), "v2": sb(C, F32), "bw": sb(K, U16),
+    "vx": sb(2 * C, F32), "val": sb(C, F32), "tab": sb(TOP + C, F32), "gj": sb(C, F32),
+    "sf": sb(K, F32), "xs": sb(K, F32), "mx": sb(K, F32), "vo": sb(K, U16), "si": sb(K, I32), "xr": sb(K, F32),
+    "pg": sb(2 * K, F32), "po": sb(2 * K, U16), "f1": sb(K, F32), "f2": sb(K, F32), "fo": sb(K, U16),
     "mf": sb(C, BF), "mw": sb(K, U16),
-    "st": sb(C, F32), "su": sb(C, F32), "sg": sb(C, BF),
-    "sw": sb(K, U16), "sf": sb(C, BF), "yf": sb(C, BF), "yw": sb(K, U16),
-    "hb": sb(4 * C, BF), "ga": sb(4 * C, BF), "rb": sb(4 * C, F32), "mb": sb(4 * C, F32), "yo": sb(C, F32),
+    "st": sb(C, F32), "su": sb(C, F32), "sg": sb(C, BF), "zm": sb(K, F32), "of": sb(K, F32),
+    "sw": sb(K, U16), "sx": sb(C, F32), "yf": sb(C, BF), "yw": sb(K, U16),
+    "hb": sb(4 * C, BF), "ga": sb(4 * C, BF), "fa": sb(4 * C, BF), "fm": sb(4 * C, BF), "rb": sb(4 * C, F32), "yo": sb(C, F32),
     "ps": ("psum", [128, 4096], F32),
 }
 for _k in range(3):
     SCRATCH["rq%d" % _k] = sb(C, MX)
     SCRATCH["rp%d" % _k] = sb(C, U8)
-for _k in range(7):
-    SCRATCH["xf%d" % _k] = sb(C, BF)
-    SCRATCH["xw%d" % _k] = sb(K, U16)
+    SCRATCH["ra%d" % _k] = sb(K, U16)
+    SCRATCH["rm%d" % _k] = sb(K, U16)
 LOADS = ["pi", "qi", "mi", "xt", "ut", "vt", "wq", "wp"]
 STORES = ["oy", "oq", "occ", "oss"]
-SEMAPHORES = ["v", "s", "t", "g"] + ["ld_" + a for a in LOADS] + ["st_" + a for a in STORES] + ["arr%d" % k for k in range(3)] + ["snt%d" % k for k in range(3)]
+SEMAPHORES = ["v", "s", "t", "g"] + ["ld_" + a for a in LOADS] + ["st_" + a for a in STORES] + [a + b + str(k) for a in ("in", "out") for b in "qam" for k in range(3)]
 
 
 def rank_program(g, core, T, topo):
@@ -81,7 +78,7 @@ def rank_program(g, core, T, topo):
             tokens |= readers.get(k, set())
         settle(e, tokens)
         s = n["sem"] or e
-        n["make"][e]().then_inc(T.sem[s], n["inc"])
+        n["make"]().then_inc(T.sem[s], n["inc"])
         count[s] = count.get(s, 0) + n["inc"]
         token = (s, count[s])
         snap[token] = dict(known[e])
@@ -91,8 +88,8 @@ def rank_program(g, core, T, topo):
 
     nodes = []
 
-    def op(e, make, rd, wr, sem=None, inc=1, cost=TINY, lat=0.0, other=None, send=None):
-        nodes.append(dict(make={e: make} if other is None else {e: make, other[0]: other[1]}, rd=rd, wr=wr, sem=sem, inc=inc, cost=cost, lat=lat, send=send))
+    def op(e, make, rd, wr, sem=None, inc=1, cost=TINY, lat=0.0, send=None):
+        nodes.append(dict(e=e, make=make, rd=rd, wr=wr, sem=sem, inc=inc, cost=cost, lat=lat, send=send))
 
     V, S = g.vector, g.scalar
 
@@ -106,18 +103,17 @@ def rank_program(g, core, T, topo):
     def cp(out, a, rd, wr, cost=TINY):
         op("v", lambda: V.tensor_copy(out, a), rd, wr, cost=cost)
 
-    def either(out, a, rd, wr, cost=GATHER):
-        op("s", lambda: S.activation(out, a, AF.Copy), rd, wr, cost=cost, other=("v", lambda: V.tensor_copy(out, a)))
-
-    def act(out, a, f, rd, wr, bias=0.0, scale=1.0, cost=GATHER):
-        if bias == 0.0 and scale == 1.0: op("s", lambda: S.activation(out, a, f), rd, wr, cost=cost)
-        else: op("s", lambda: S.activation(out, a, f, bias=bias, scale=scale), rd, wr, cost=PLAIN)
+    def act(out, a, rd, wr, cost=GATHER, **how):
+        op("s", lambda: S.activation(out, a, AF.Identity if how else AF.Copy, **how), rd, wr, cost=cost)
 
     def scan(out, a, b, init, o0, o1, rd, wr, cost=PLAIN):
         op("v", lambda: V.tensor_tensor_scan(out, a, b, init, o0, o1), rd, wr, cost=cost)
 
     def load(e, name, out, in_):
         op(e, lambda: queue[e].dma_start(out, in_), [], [name], "ld_" + name, 16, cost=0.1, lat=2.5)
+
+    def store(e, name, out, in_, rd):
+        op(e, lambda: queue[e].dma_start(out, in_), rd, [], "st_" + name, 16, cost=0.1, lat=2.5)
 
     def ordered():
         wrote, read, preds, succ = {}, {}, [], []
@@ -136,40 +132,45 @@ def rank_program(g, core, T, topo):
             for j in p: succ[j].append(i)
         rank_ = [0.0] * len(nodes)
         for i in range(len(nodes) - 1, -1, -1):
-            rank_[i] = nodes[i]["cost"] + nodes[i]["lat"] + max([rank_[j] + WAKE for j in succ[i]] + [0.0])
-        free, at, end, todo = {e: 0.0 for e in queue}, {}, {}, [len(p) for p in preds]
-        open_, out = [i for i in range(len(nodes)) if not preds[i]], []
+            rank_[i] = (EARLY if EAGER & set(nodes[i]["wr"]) else 0.0) + nodes[i]["cost"] + nodes[i]["lat"] + max([rank_[j] + (NEAR if nodes[j]["e"] == nodes[i]["e"] else WAKE) for j in succ[i]] + [0.0])
+        free, end, todo = {e: 0.0 for e in queue}, {}, [len(p) for p in preds]
+        ready, open_, out = {}, [i for i in range(len(nodes)) if not preds[i]], []
+        for i in open_: ready[i] = 0.0
         while open_:
-            best, spots = {}, {}
-            waiting = min([max([end[j] + (NEAR if at[j] == "v" else WAKE) for j in preds[i]] + [0.0]) for i in open_ if list(nodes[i]["make"]) == ["v"]] + [1e9])
-            for i in open_:
-                spot = None
-                for e in nodes[i]["make"]:
-                    r = max([end[j] + (NEAR if at[j] == e else WAKE) for j in preds[i]] + [0.0])
-                    t = max(r, free[e])
-                    a = (t + (BIAS if e == "v" and len(nodes[i]["make"]) > 1 and waiting < t + GATHER * LOOK else 0.0), e, r)
-                    if spot is None or a < spot: spot = a
-                spots[i] = spot
-                e, r = spot[1], max(spot[2], free[spot[1]])
-                best[e] = min(best.get(e, 1e9), r)
-            e = min(best, key=lambda a: (best[a], a))
-            i = max([j for j in open_ if spots[j][1] == e and max(spots[j][2], free[e]) <= best[e] + SLACK], key=lambda j: (rank_[j], -j))
-            t = max(spots[i][2], free[e])
-            free[e], at[i], end[i] = t + nodes[i]["cost"], e, t + nodes[i]["cost"] + nodes[i]["lat"]
+            start = {i: max(ready[i], free[nodes[i]["e"]]) for i in open_}
+            soon = min(open_, key=lambda i: (start[i], i))
+            e = nodes[soon]["e"]
+            due = [j for j in open_ if nodes[j]["e"] == e]
+            i = max([j for j in due if start[j] <= start[soon] + SLACK], key=lambda j: (rank_[j], -j))
+            for j in sorted(due, key=lambda j: -rank_[j]):
+                if start[i] < start[j] < start[i] + nodes[i]["cost"] and rank_[j] - rank_[i] > nodes[j]["cost"] + 2 * (start[j] - start[i]) + YIELD:
+                    small = [a for a in due if start[a] + nodes[a]["cost"] <= start[j] + SLACK]
+                    i = max(small, key=lambda a: (rank_[a], -a)) if small else j
+                    break
+            free[e], end[i] = start[i] + nodes[i]["cost"], start[i] + nodes[i]["cost"] + nodes[i]["lat"]
             open_.remove(i)
-            out.append((nodes[i], e))
+            out.append((nodes[i], e, start[i]))
             for j in succ[i]:
                 todo[j] -= 1
-                if not todo[j]: open_.append(j)
+                if not todo[j]:
+                    open_.append(j)
+                    ready[j] = max([end[a] + (NEAR if nodes[a]["e"] == nodes[j]["e"] else WAKE) for a in preds[j]])
         return out
 
-    def held(name):
-        scan(T.ex[:], T.hc[:], T[name][:], 0.0, O.add, O.max, ["hc", name], ["ex"])
-        return T.ex[:, 15:C:16]
+    def held(name, key, out):
+        scan(T[out][:], T.hc[:], name, 0.0, O.add, O.max, ["hc", key], [out])
+        return T[out][:, 15:C:16]
 
-    def unwrap(name, n, w, more=[]):
-        scan(T.eh[:, 0:n], T.hh[:, 0:n], T[name][:, 0:n], 0.0, O.add, O.max, ["hh", name] + more, ["eh"], HALF * n / C)
-        ts(T[w][:, 0:n // 16], T.eh[:, 15:n:16], T.coh[:, 0:1], None, O.subtract, None, ["eh", "coh"], [w])
+    def short(name):
+        scan(T.eh[:], T.hh[:], T[name][:], 0.0, O.add, O.max, ["hh", name], ["eh"], HALF)
+        return T.eh[:, 15:C:16]
+
+    def unwrap(name, w):
+        ts(T[w][:], short(name), T.coh[:, 0:1], None, O.subtract, None, ["eh", "coh"], [w])
+
+    def pointers(name, w, out):
+        scan(T[out][:], T[name][:], T.kr[:], DROP, O.max, O.add, ["kr", name], [out])
+        ts(T[w][:], T[out][:, 15:C:16], T.c72[:, 0:1], 1.0 / UNIT, O.subtract, O.mult, [out, "c72"], [w])
 
     def bank(b, n=C):
         return T.ps[:, 512 * b:512 * b + n]
@@ -179,237 +180,189 @@ def rank_program(g, core, T, topo):
            [r, rs] + ([key] if key else [l, ls]), ["ps%d" % b], cost=0.3)
 
     def quant(q, p, t, n, rd=None):
-        op("v", lambda: V.quantize_mx(T[q][:, 0:n], T[p][:, 0:n], T[t][:, 0:4 * n]), rd or [t], [q, p], cost=0.32)
+        op("v", lambda: V.quantize_mx(T[q][:, 0:n], T[p][:, 0:n], T[t][:, 0:4 * n]), rd or [t], [q, p], cost=0.32 * n / C)
 
     def iota(name, out, pattern, base, mul, small=True):
-        cost = 0.14 + 0.002 * (C if len(pattern) > 1 else pattern[0][1])
+        cost = 0.14 + 0.002 * pattern[0][1]
         if small: op("g", lambda: g.iota(out, pattern, base, mul, allow_small_or_imprecise_dtypes=True), [], [name], cost=cost)
         else: op("g", lambda: g.iota(out, pattern, base, mul), [], [name], cost=cost)
 
-    load("y", "pi", T.pi[:], T.pl[:])
-    load("s", "qi", T.qi[:], T.ql[:])
-    load("y", "xt", T.xt[:], T.x[:])
+    def send(k, kind, pairs, lat):
+        peer = T.cores[rank ^ STEPS[k]]
+        rid, pid = topo.addr(peer, core)
+        mask, n = topo.mask(core, peer), len(topo.engines(core, peer)) * len(pairs)
+        land, sent = "in%s%d" % (kind, k), "out%s%d" % (kind, k)
+
+        def go():
+            settle("g", {last[a] for a, x, b, y in pairs})
+            for a, x, b, y in pairs:
+                g.remote_dma(y, x, T.sem[land], T.sem[sent], pid, rid, mask)
+                readers.setdefault(a, set()).add((sent, n))
+                last[b] = (land, n)
+            count[land] = count[sent] = n
+
+        op("g", None, [a for a, x, b, y in pairs], [b for a, x, b, y in pairs], cost=0.3 * len(pairs), lat=lat, send=go)
+
+    def part(name, b):
+        return T[name][:, C * b:C * b + C]
+
+    load("y", "qi", T.qi[:], T.ql[:])
+    load("s", "xt", T.xt[:], T.x[:])
     load("y", "ut", T.ut[:], T.u[:])
+    load("y", "pi", T.pi[:], T.pl[:])
     load("y", "mi", T.mi[:], T.ml[:])
     load("y", "wq", T.wq[:].bitcast(dt.uint8), T.wc[:])
     load("y", "wp", T.wp[:], T.ws[:])
     load("y", "vt", T.vt[:], T.v[:])
 
+    iota("di", T.di[:], [[1, K]], 129, -1, False)
     iota("pp", T.pp[:], [[1, 1]], 0, 1, False)
-    iota("tm", T.tm[:], [[0, K], [1, 16]], 0, 0)
-    iota("cc", T.cc[:, 0:C], [[1, C]], -MID, 0)
-    iota("wm0", T.wm0[:], [[UNIT, C]], LIFT + SEEN - 1, 0)
-    iota("w0", T.w0[:], [[UNIT, C]], LIFT + SEEN, 0)
-    iota("ou0", T.ou0[:], [[16, 8]], 0, 0, False)
     iota("cw0", T.cw0[:], [[16, K]], 0, 0)
-    op("v", lambda: V.memset(T.one[:], 1.0), [], ["one"])
-    for b in range(4):
-        op("g", lambda b=b: g.affine_select(T.et[:, 512 * b:512 * b + 512], T.one[:], [[-1, 512]], O.is_equal, 0.0, b, 4), ["one"], ["et%d" % b], cost=1.2)
-    iota("cd", T.cd[:], [[UNIT, C]], LIFT - 1, 0)
+    iota("ou0", T.ou0[:], [[16, 8]], 0, 0, False)
+    iota("cf", T.cf[:], [[1, C]], 0, 0)
+    op("v", lambda: V.memset(T.one[:], 1.0), [], ["one"], cost=0.27)
+    op("g", lambda: g.affine_select(T.et[:], T.one[:], [[-1, 516]], O.is_equal, 0.0, 3, 4), ["one"], ["et"], cost=1.2)
+    ts(T.dm[:], T.di[:], 15, None, O.bitwise_and, None, ["di"], ["dm"])
+    ts(T.ka[:], T.dm[:], 1.0, DROP, O.is_equal, O.mult, ["dm"], ["ka"])
+    ts(T.kb[:], T.dm[:], 2.0, HOLD, O.is_equal, O.mult, ["dm"], ["kb"])
+    tt(T.kc[:], T.ka[:, 0:16], T.kb[:, 0:16], O.add, ["ka", "kb"], ["kc"])
+    tt(T.kd[:], T.ka[:, 1:17], T.kb[:, 1:17], O.add, ["ka", "kb"], ["kd"])
     ts(T.pm[:], T.pp[:], 15, None, O.bitwise_and, None, ["pp"], ["pm"])
     cp(T.pf[:], T.pm[:], ["pm"], ["pf"])
+    ts(T.iw[:], T.cw0[:], 0.0, T.pf[:, 0:1], O.mult, O.add, ["cw0", "pf"], ["iw"])
+    act(T.kr[:], T.kd[:].indirect(T.iw[:]), ["kd", "iw"], ["kr"])
+    act(T.cu[:], T.cw0[:], ["cw0"], ["cu"], TINY, scale=float(UNIT))
+    tt(T.kr[:, 15:C:16], T.kr[:, 15:C:16], T.cu[:], O.add, ["cu"], ["kr"])
+    act(T.hc[:], T.kc[:].indirect(T.iw[:]), ["kc", "iw"], ["hc"])
+    act(T.hh[:], T.hc[:], ["hc"], ["hh"], PLAIN, scale=2.0 ** -10)
+    act(T.ku[:], T.cf[:], ["cf"], ["ku"], PLAIN, scale=-float(UNIT), bias=1.0)
+    act(T.vx[:, 0:C], T.cf[:], ["cf"], ["vc"], PLAIN, bias=float(TOP + LEN))
+    act(T.tab[:, TOP:TOP + C], T.cf[:], ["cf"], ["tc"], PLAIN, bias=float(TOP + LEN))
     ts(T.cor[:], T.pf[:], 15.0, HOLD, O.is_lt, O.mult, ["pf"], ["cor"])
-    ts(T.dif[:], T.tm[:], T.pf[:, 0:1], None, O.subtract, None, ["tm", "pf"], ["dif"])
-    ts(T.ka[:], T.dif[:], 0.0, DROP, O.is_equal, O.mult, ["dif"], ["ka"])
-    ts(T.kb[:], T.dif[:], 1.0, HOLD, O.is_equal, O.mult, ["dif"], ["kb"])
-    tt(T.hc[:], T.ka[:], T.kb[:], O.add, ["ka", "kb"], ["hc"])
-    ts(T.hh[:, 0:C], T.hc[:], 2.0 ** -10, None, O.mult, None, ["hc"], ["hh"])
-    ts(T.coh[:], T.cor[:], 2.0 ** -10, float(MID), O.mult, O.subtract, ["cor"], ["coh"])
+    ts(T.cn0[:], T.pf[:], 0.0, DROP, O.is_equal, O.mult, ["pf"], ["cn0"])
+    act(T.cn1[:], T.pf[:], ["pf", "cn0"], ["cn1"], TINY, scale=-float(UNIT), bias=T.cn0[:, 0:1])
+    for name, of, scale, bias in (("con", "cn1", 1.0, HOLD), ("c72", "cn1", 1.0, HOLD + 72), ("c73", "cor", 1.0, 73), ("cln", "cor", 1.0, LEN), ("co2", "cor", 2.0, LEN),
+                                  ("cov", "cor", 2.0, LEN + TOP - C), ("ctp", "cor", 2.0, LEN + TOP), ("coh", "cor", 2.0 ** -10, -MID)):
+        act(T[name][:], T[of][:], [of], [name], TINY, scale=scale, bias=float(bias))
+    act(T.cw[:], T.cw0[:], ["cw0", "pf"], ["cw"], TINY, bias=T.pf[:, 0:1])
+    act(T.kst[:], T.cw[:], ["cw", "con"], ["kst"], TINY, scale=float(UNIT), bias=T.con[:, 0:1])
+    act(T.kx[:], T.cw[:], ["cw", "ctp"], ["kx"], TINY, bias=T.ctp[:, 0:1])
+    act(T.kx2[:], T.cw[:], ["cw", "cov"], ["kx2"], TINY, bias=T.cov[:, 0:1])
+    cp(T.ou[:], T.ou0[:], ["ou0"], ["ou"])
 
     cp(T.qw[:], T.qi[:], ["qi"], ["qw"])
     cp(T.pw[:], T.pi[:], ["pi"], ["pw"])
-    act(T.qa[:], T.cc[:, 0:C].indirect(T.qw[:]), AF.Copy, ["cc", "qw"], ["qa"])
-    act(T.xf0[:], T.qa[:].indirect(T.pw[:]), AF.Copy, ["qa", "pw"], ["xf0"])
-    op("v", lambda: V.memset(T.ones[:], 1.0), [], ["ones"], cost=PLAIN)
-    op("v", lambda: V.memset(T.buf[:, 0:8], 0.0), [], ["buf"])
-    cp(T.cc[:, C:2 * C], T.cc[:, 0:C], ["cc"], ["cd2"], HALF)
-    cp(T.hh[:, C:2 * C], T.hh[:, 0:C], ["hh"], ["hh2"], HALF)
-    cp(T.ou[:], T.ou0[:], ["ou0"], ["ou"])
+    act(T.qa[:], T.cf[:].indirect(T.qw[:]), ["cf", "qw"], ["qa"], scale=float(UNIT))
+    tt(T.dmw[:], T.mi[:], T.cw[:], O.subtract, ["mi", "cw"], ["dmw"])
+    ts(T.muf[:], T.dmw[:], T.cor[:, 0:1], 2.0 ** -10, O.mult, O.mult, ["dmw", "cor"], ["muf"])
+    tt(T.cq[:], T.cw[:], T.muf[:], O.subtract, ["cw", "muf"], ["cq"])
+    for w, o in (("low", O.min), ("hiw", O.max)):
+        tt(T.muf[:], T.mi[:], T.cw[:], o, ["mi", "cw"], ["muf"])
+        cp(T[w][:], T.muf[:], ["muf"], [w])
 
-    def jump():
-        unwrap("xf0", C, "xw0")
-        w, wm, made = "w0", "wm0", 0
-        for n, (k, s) in enumerate(JUMPS):
-            if n:
-                act(T.wm[:], T[w][:], AF.Identity, [w], ["wm"], bias=-float(s))
-                wm = "wm"
-            nxt = "wb" if w == "wa" else "wa"
-            tt(T[nxt][:], T[w][:].indirect(T["xw%d" % k][:]), T[wm][:], O.min, [w, "xw%d" % k, wm], [nxt], GATHER)
-            w = nxt
-            if made == k and k < 6:
-                either(T["xf%d" % (k + 1)][:], T["xf%d" % k][:].indirect(T["xw%d" % k][:]), ["xf%d" % k, "xw%d" % k], ["xf%d" % (k + 1)])
-                unwrap("xf%d" % (k + 1), C, "xw%d" % (k + 1))
-                made = k + 1
-        tt(T.dd[:], T[w][:].indirect(T.xw0[:]), T.cd[:], O.subtract, [w, "xw0", "cd"], ["dd"], GATHER)
-        for a, c in (("c5", 2.0), ("ctr", 1.0)):
-            op("s", lambda a=a, c=c: S.activation(T[a][:], T.dd[:], AF.Relu, scale=c), ["dd"], [a], cost=PLAIN,
-               other=("v", lambda a=a, c=c: V.tensor_scalar(T[a][:], T.dd[:], 0.0, c, O.max, O.mult)))
-        a = held(w)
-        ts(T.lw[:], a, T.cor[:, 0:1], 1.0 / UNIT, O.subtract, O.mult, ["ex", "cor"], ["lw"])
-        ts(T.vi[:], a, T.cor[:, 0:1], float(LIFT), O.subtract, O.subtract, ["ex", "cor"], ["vi"])
-        scan(T.buf[:, 1:C + 1], T.ones[:, 0:C], T.c5[:], 0.0, O.mult, O.add, ["ones", "c5"], ["buf"])
-        either(T.bg[:], T.buf[:, 0:C].indirect(T.lw[:]), ["buf", "lw"], ["bg"])
-        ts(T.tw[:], T.vi[:], UNIT - 1, None, O.bitwise_and, None, ["vi"], ["tw"])
-        ts(T.t2[:], T.tw[:], T.cor[:, 0:1], None, O.subtract, None, ["tw", "cor"], ["t2"])
-        either(T.lg[:], T.ctr[:].indirect(T.lw[:]), ["ctr", "lw"], ["lg"])
-        scan(T.eh[:, 0:C], T.hh[:, 0:C], T.lg[:], 0.0, O.add, O.max, ["hh", "lg"], ["eh"], HALF)
-        ts(T.ll[:], T.eh[:, 15:C:16], T.coh[:, 0:1], float(MID), O.subtract, O.subtract, ["eh", "coh"], ["ll"])
-        a = held("bg")
-        tt(T.ps2[:, 0:K], a, T.t2[:], O.add, ["ex", "t2"], ["psa"])
-        tt(T.ps2[:, K:2 * K], T.ps2[:, 0:K], T.ll[:, 0:K], O.add, ["psa", "ll"], ["psb"])
-        cp(T.pos[:], T.ps2[:], ["psa", "psb"], ["pos"])
-        cp(T.lin[:].indirect(T.pos[:]), T.cc[:], ["pos", "cc", "cd2"], ["lin"], SCATTER)
-        for a, w in ((0, "lca"), (K, "lcb")): ts(T.lc[:, a:a + K], T.ll[:], T.coj[:, 0:1], None, O.add, None, ["ll", "coj"], [w])
-        ts(T.posr[:], T.ps2[:, 0:K], -1.0, float(2 * C - 1), O.mult, O.add, ["psa"], ["posr"])
-        unwrap("lin", 2 * C, "linw", ["hh2"])
+    def ahead(k, q):
+        tt(T.arl[:], T[q][:].indirect(T.pw[:]), T.ku[:], O.add, [q, "pw", "ku"], ["arl"], GATHER)
+        act(T.aab[:], T[q][:].indirect(T.pw[:]), [q, "pw"], ["aab"], bias=1.0)
+        pointers("arl", "aw", "exa")
+        send(k, "a", [("aw", T.aw[:], "ra%d" % k, T["ra%d" % k][:])], HOP)
 
-    def products():
+    def state(k):
         mm(4, "ur", "urp", 0, "tq", "tp")
+        send(k, "q", [("tq", T.tq[:].bitcast(dt.uint8), "rq%d" % k, T["rq%d" % k][:].bitcast(dt.uint8)), ("tp", T.tp[:], "rp%d" % k, T["rp%d" % k][:])], FLIGHT)
         for b in range(4): mm(b, "eq", "ep", 128 * b, "tq", "tp", "eq%d" % b)
 
-    def times(out, a, c, rd, wr):
-        op("s", lambda: S.activation(out, a, AF.Identity, scale=c), rd, wr, cost=PLAIN, other=("v", lambda: V.tensor_scalar(out, a, c, None, O.mult)))
-
-    def halves():
-        for b in range(4): times(T.hb[:, C * b:C * b + C], bank(b), 0.5, [], ["ps%d" % b, "hb%d" % b])
-
-    def aside():
-        for b in range(4):
-            either(T.ga[:, b:4 * C:4], T.hb[:, C * b:C * b + C].indirect(T.xw0[:]), ["hb%d" % b, "xw0"], ["ga%d" % b])
-
-    def prepare():
-        ts(T.hm[:], T.hh[:], 2.0, None, O.mult, None, ["hh", "hh2"], ["hm"], PLAIN)
-        ts(T.coj[:], T.cor[:], 2.0 ** -9, None, O.mult, None, ["cor"], ["coj"])
-
-    def prepare2():
-        ts(T.cw[:], T.cw0[:], T.pf[:, 0:1], None, O.add, None, ["cw0", "pf"], ["cw"])
-        tt(T.dmw[:], T.mi[:], T.cw[:], O.subtract, ["mi", "cw"], ["dmw"])
-        ts(T.muf[:], T.dmw[:], T.cor[:, 0:1], 2.0 ** -10, O.mult, O.mult, ["dmw", "cor"], ["muf"])
-        tt(T.cq[:], T.cw[:], T.muf[:], O.subtract, ["cw", "muf"], ["cq"])
-        for w, o in (("low", O.min), ("hiw", O.max)):
-            tt(T.muf[:], T.mi[:], T.cw[:], o, ["mi", "cw"], ["muf"])
-            cp(T[w][:], T.muf[:], ["muf"], [w])
-
-    def first():
-        quant("uq", "up", "ut", 128)
-        cp(T.ur[:].bitcast(dt.uint32), T.uq[:].bitcast(dt.uint32).indirect(T.ou[:]), ["uq", "ou"], ["ur"])
-        cp(T.urp[:], T.up[:].indirect(T.ou[:]), ["up", "ou"], ["urp"])
-        quant("tq", "tp", "xt", C)
-
-    def constants():
-        for b in range(4):
-            op("v", lambda b=b: V.quantize_mx(T.eq[:, 128 * b:128 * b + 128], T.ep[:, 128 * b:128 * b + 128], T.et[:, 512 * b:512 * b + 512]), ["et%d" % b], ["eq%d" % b], cost=0.15)
-        products()
-
-    first()
-    constants()
-    prepare()
-    prepare2()
-    jump()
+    quant("uq", "up", "ut", 128)
+    cp(T.ur[:].bitcast(dt.uint32), T.uq[:].bitcast(dt.uint32).indirect(T.ou[:]), ["uq", "ou"], ["ur"], 0.25)
+    op("s", lambda: S.activation(T.urp[:], T.up[:].indirect(T.ou[:]), AF.Copy), ["up", "ou"], ["urp"], cost=0.25)
+    quant("tq", "tp", "xt", C)
+    for b in range(4):
+        op("v", lambda b=b: V.quantize_mx(T.eq[:, 128 * b:128 * b + 128], T.ep[:, 128 * b:128 * b + 128], T.et[:, 3 - b:515 - b]), ["et"], ["eq%d" % b], cost=0.15)
     quant("vq", "vp", "vt", 128)
+    state(0)
+    ahead(0, "qa")
 
     qcur = ["qa", "qb"]
-    for k, step in enumerate(STEPS):
-        final = k == 2
-        peer = T.cores[rank ^ step]
-        rid, pid = topo.addr(peer, core)
-        mask = topo.mask(core, peer)
-        width = len(topo.engines(core, peer))
+    for k in range(len(STEPS)):
+        final = k == len(STEPS) - 1
         ts(T.nf[:], bank(4), 0.0, None, O.is_ge, None, [], ["ps4", "nf"], PLAIN)
-        cp(T.g2[:, 0:16 * CUT], T.nf[:].indirect(T.linw[:, 0:CUT]), ["nf", "linw"], ["g2a"], GATHER * CUT / K)
-        act(T.g2[:, 16 * CUT:2 * C], T.nf[:].indirect(T.linw[:, CUT:2 * K]), AF.Copy, ["nf", "linw"], ["g2b"], cost=GATHER * (2 * K - CUT) / K)
-        act(T.ss[:], bank(4), AF.Copy, [], ["ps4", "ss"], cost=PLAIN)
-        scan(T.fs[:], T.g2[:], T.ones[:], 1.0, O.mult, O.add, ["g2a", "g2b", "ones"], ["fs"])
-        act(T.ij[:, 0:C], T.fs[:].indirect(T.pos[:, K:2 * K]), AF.Copy, ["fs", "pos"], ["ija"])
-        scan(T.rs[:], T.g2[:, ::-1], T.ones[:], 1.0, O.mult, O.add, ["g2a", "g2b", "ones"], ["rs"])
-        cp(T.ij[:, C:2 * C], T.rs[:].indirect(T.posr[:]), ["rs", "posr"], ["ijb"], GATHER)
-        halves()
-        aside()
-        scan(T.eij[:], T.hm[:], T.ij[:], 0.0, O.add, O.max, ["hm", "ija", "ijb"], ["eij"])
-        tt(T.k3[:], T.eij[:, 15:2 * C:16], T.lc[:], O.min, ["eij", "lca", "lcb"], ["k3"])
-        tt(T.de[:], T.k3[:, K:2 * K], T.k3[:, 0:K], O.subtract, ["k3"], ["de"])
-        ts(T.zl[:], T.de[:], 0.0, None, O.is_lt, None, ["de"], ["zl"])
-        tt(T.dp[:], T.de[:], T.ps2[:, 0:K], O.add, ["de", "psa"], ["dp"])
-        tt(T.zm[:], T.zl[:], T.ll[:, 0:K], O.mult, ["zl", "ll"], ["zm"])
-        tt(T.of[:], T.zm[:], T.dp[:], O.add, ["zm", "dp"], ["of"])
-        cp(T.ow[:], T.of[:], ["of"], ["ow"])
-        either(T.mf[:], T.lin[:].indirect(T.ow[:]), ["lin", "ow"], ["mf"])
-        unwrap("mf", C, "mw")
-        act(T.st[:], T.ss[:].indirect(T.mw[:]), AF.Copy, ["ss", "mw"], ["st"])
-        act(T.su[:], T.st[:].indirect(T.low[:]), AF.Copy, ["st", "low"], ["su"])
-        parts = [(0, 8), (8, K)] if final else [(0, K)]
-        for h, (a, z) in enumerate(parts):
-            own = [h] if final else [0, 1]
-            zs = ["zt%d%d" % (j, b) for b in range(4) for j in own]
-            for b in range(4):
-                tt(T.zt[:, 64 * a + b:64 * z:4], T.hb[:, C * b:C * b + C].indirect(T.mw[:, a:z]), T.ga[:, 64 * a + b:64 * z:4], O.add, ["hb%d" % b, "mw", "ga%d" % b], ["zt%d%d" % (j, b) for j in own], GATHER * (z - a) / K)
-            op("v", lambda a=a, z=z: V.quantize_mx(T.zq[:, 16 * a:16 * z], T.zp[:, 16 * a:16 * z], T.zt[:, 64 * a:64 * z]), zs, ["zq0", "zq1"][h:], cost=0.32 * (z - a) / K)
-
-            def send(k=k, pid=pid, rid=rid, mask=mask, a=16 * a, z=16 * z, h=h, n=2 * width * len(parts)):
-                settle("g", {last["zq%d" % h]})
-                land, sent = T.sem["arr%d" % k], T.sem["snt%d" % k]
-                g.remote_dma(T["rq%d" % k][:, a:z].bitcast(dt.uint8), T.zq[:, a:z].bitcast(dt.uint8), land, sent, pid, rid, mask)
-                g.remote_dma(T["rp%d" % k][:, a:z], T.zp[:, a:z], land, sent, pid, rid, mask)
-                readers.setdefault("zq%d" % h, set()).add(("snt%d" % k, n))
-                for r in ("rq%d" % k, "rp%d" % k): last[r] = ("arr%d" % k, n)
-                count["arr%d" % k] = count["snt%d" % k] = n
-
-            op("g", None, ["zq%d" % h], ["rq%d" % k, "rp%d" % k], cost=0.6, lat=FLIGHT, send=send)
+        act(T.ss[:], bank(4), [], ["ps4", "ss"], PLAIN)
+        tt(T.v0[:], T.nf[:], T.arl[:], O.mult, ["nf", "arl"], ["v0"], BOTH)
+        for b in range(4): act(part("fa", b), bank(b), [], ["ps%d" % b, "fa%d" % b], PLAIN, scale=32.0 if b in TURNED else 1.0)
+        for b, at in enumerate((5, 6, 7, 4)):
+            mm(at, "eq", "ep", 128 * b, "rq%d" % k, "rp%d" % k, "eq%d" % b)
+            act(part("hb", b), bank(at), [], ["ps%d" % at, "hb%d" % b], PLAIN, scale=0.5)
+            act(T.ga[:, b:4 * C:4], part("hb", b).indirect(T["ra%d" % k][:]), ["hb%d" % b, "ra%d" % k], ["ga%d" % b])
+        base = "v0"
+        for n, r in enumerate(RADIX):
+            pointers(base, "bw", "ex" if n else "ex1")
+            act(T.v2[:], T[base][:], [base], ["v2"], PLAIN)
+            for j in range(r - 1):
+                nxt = "v1" if base == "v0" else "v0"
+                tt(T[nxt][:], T[base][:].indirect(T.bw[:]), T.v2[:], O.add, [base, "v2", "bw"], [nxt], GATHER)
+                base = nxt
+        tt(T.vx[:, C:2 * C], T[base][:].indirect(T.aw[:]), T.aab[:], O.add, [base, "aw", "aab"], ["vx"], GATHER)
+        tt(T.sf[:], T.ex1[:, 15:C:16], T.kst[:], O.is_equal, ["ex1", "kst"], ["sf"])
+        tt(T.xs[:], T.sf[:], T.kx[:], O.mult, ["sf", "kx"], ["xs"])
+        tt(T.mx[:], T.xs[:], T.kx2[:], O.max, ["xs", "kx2"], ["mx"])
+        ts(T.vo[:], T.mx[:], T.cov[:, 0:1], None, O.subtract, None, ["mx", "cov"], ["vo"])
+        act(T.val[:], T.vx[:].indirect(T.vo[:]), ["vx", "vc", "vo"], ["val"])
+        a = held(T.vx[:, C:2 * C], "vx", "ex")
+        ts(T.si[:], a, T.c73[:, 0:1], 1.0 / UNIT, O.subtract, O.mult, ["ex", "c73"], ["si"])
+        tt(T.xr[:], a, T.xs[:], O.add, ["ex", "xs"], ["xr"])
+        ts(T.pg[:, K:2 * K], T.si[:], float(UNIT), T.cln[:, 0:1], O.mult, O.add, ["si", "cln"], ["pgb"])
+        tt(T.pg[:, 0:K], T.pg[:, K:2 * K], T.xr[:], O.min, ["pgb", "xr"], ["pga"])
+        ts(T.po[:], T.pg[:], T.cor[:, 0:1], None, O.subtract, None, ["pga", "pgb", "cor"], ["po"])
+        cp(T.tab[:].indirect(T.po[:, 0:K]), T.val[:], ["po", "val", "tc"], ["tab"], SCATTER)
+        tt(T.gj[:], T.tab[:].indirect(T.po[:, K:2 * K]), T.vx[:, C:2 * C], O.subtract, ["tab", "po", "vx"], ["gj"], GATHER)
+        a = held(T.gj[:], "gj", "ex")
+        tt(T.f1[:], a, T.pg[:, K:2 * K], O.add, ["ex", "pgb"], ["f1"])
+        tt(T.f2[:], T.f1[:], T.xs[:], O.max, ["f1", "xs"], ["f2"])
+        ts(T.fo[:], T.f2[:], T.co2[:, 0:1], None, O.subtract, None, ["f2", "co2"], ["fo"])
+        ts(T.mf[:], T.tab[:].indirect(T.fo[:]), float(TOP + LEN + MID), None, O.subtract, None, ["tab", "fo"], ["mf"], GATHER)
+        unwrap("mf", "mw")
+        send(k, "m", [("mw", T.mw[:], "rm%d" % k, T["rm%d" % k][:])], HOP)
+        act(T.st[:], T.ss[:].indirect(T.mw[:]), ["ss", "mw"], ["st"])
+        act(T.su[:], T.st[:].indirect(T.low[:]), ["st", "low"], ["su"])
         tt(T.sg[:], T.st[:].indirect(T.hiw[:]), T.su[:], O.is_lt, ["st", "hiw", "su"], ["sg"], GATHER)
-        scan(T.eh[:, 0:C], T.hh[:, 0:C], T.sg[:], 0.0, O.add, O.max, ["hh", "sg"], ["eh"], HALF)
-        tt(T.zm[:], T.eh[:, 15:C:16], T.dmw[:], O.mult, ["eh", "dmw"], ["zm"])
+        tt(T.zm[:], short("sg"), T.dmw[:], O.mult, ["eh", "dmw"], ["zm"])
         tt(T.of[:], T.zm[:], T.cq[:], O.add, ["zm", "cq"], ["of"])
         cp(T.sw[:], T.of[:], ["of"], ["sw"])
         qo, qn = qcur[k % 2], qcur[1 - k % 2]
-        either(T.yf[:], T[qo][:].indirect(T.sw[:]), [qo, "sw"], ["yf"])
-        either(T.sf[:], T.cc[:, 0:C].indirect(T.sw[:]), ["cc", "sw"], ["sf"])
-        unwrap("yf", C, "yw")
-        either(T[qn][:], T.sf[:].indirect(T.yw[:]), ["sf", "yw"], [qn])
-        if not final:
-            either(T.xf0[:], T[qn][:].indirect(T.pw[:]), [qn, "pw"], ["xf0"])
+        act(T.yf[:], T[qo][:].indirect(T.sw[:]), [qo, "sw"], ["yf"], scale=1.0 / UNIT, bias=-float(MID))
+        act(T.sx[:], T.cf[:].indirect(T.sw[:]), ["cf", "sw"], ["sx"])
+        unwrap("yf", "yw")
+        if final:
+            act(T[qn][:], T.sx[:].indirect(T.yw[:]), ["sx", "yw"], [qn])
+            store("y", "oq", T.qo[:], T[qn][0:128:16, :], [qn])
         else:
-            ts(T.dd[:], T[qn][:], float(MID), None, O.add, None, [qn], ["dd"], PLAIN)
-            op("y", lambda: g.sync.dma_start(T.qo[:], T.dd[0:128:16, :]), ["dd"], [], "st_oq", 16, lat=2.5)
-
-        def layer():
-            for b in range(4): mm((5, 6, 7, 4)[b], "wq", "wp", 128 * b, "rq%d" % k, "rp%d" % k)
-
-        def scaled(bs):
-            for b in bs:
-                times(T.rb[:, C * b:C * b + C], bank((5, 6, 7, 4)[b]), 0.03125, [], ["ps%d" % (5, 6, 7, 4)[b], "rb%d" % b])
-
-        def picked(bs):
-            for b in bs:
-                either(T.mb[:, C * b:C * b + C], T.rb[:, C * b:C * b + C].indirect(T.mw[:]), ["rb%d" % b, "mw"], ["mb%d" % b])
-
-        def added(bs=range(4)):
-            for b in bs:
-                tt(T.xt[:, b:4 * C:4], T.mb[:, C * b:C * b + C], bank(b), O.add, ["mb%d" % b], ["ps%d" % b, "xt%d" % b], PLAIN)
-            quant("tq", "tp", "xt", C, ["xt", "xt0", "xt1", "xt2", "xt3"])
-
+            act(T[qn][:], T.sx[:].indirect(T.yw[:]), ["sx", "yw"], [qn], scale=float(UNIT))
+            ahead(k + 1, qn)
+        for b in range(4):
+            tt(T.zt[:, b:4 * C:4], part("hb", b).indirect(T["rm%d" % k][:]), T.ga[:, b:4 * C:4], O.add, ["hb%d" % b, "rm%d" % k, "ga%d" % b], ["zt%d" % b], GATHER)
+        quant("zq", "zp", "zt", C, ["zt0", "zt1", "zt2", "zt3"])
+        for b in TURNED: act(part("fm", b), part("fa", b).indirect(T.mw[:]), ["fa%d" % b, "mw"], ["fm%d" % b])
+        for b in (FUSED[0], TURNED[0], FUSED[1], TURNED[1]): mm(b, "wq", "wp", 128 * b, "zq", "zp")
+        for b in FUSED:
+            act(part("rb", b), bank(b), [], ["ps%d" % b, "rb%d" % b], PLAIN, scale=0.03125)
+            tt(T.xt[:, b:4 * C:4], part("rb", b).indirect(T.mw[:]), part("fa", b), O.add, ["rb%d" % b, "mw", "fa%d" % b], ["xt%d" % b], GATHER)
+        for b in TURNED:
+            tt(part("rb", b), bank(b), part("fm", b), O.add, ["fm%d" % b], ["ps%d" % b, "rb%d" % b], PLAIN)
+            act(T.xt[:, b:4 * C:4], part("rb", b).indirect(T.mw[:]), ["rb%d" % b, "mw"], ["xt%d" % b], scale=0.03125)
+        quant("tq", "tp", "xt", C, ["xt", "xt0", "xt1", "xt2", "xt3"])
         if not final:
-            layer()
-            scaled(range(4))
-            picked(range(4))
-            added()
-            products()
-            jump()
+            state(k + 1)
         else:
-            layer()
-            for b in (0, 1):
-                cp(T.mb[:, C * b:C * b + C], bank(b), [], ["ps%d" % b, "mb%d" % b], PLAIN)
-            scaled(range(4))
-            picked([2, 3])
-            for b in (0, 1):
-                tt(T.xt[:, b:4 * C:4], T.rb[:, C * b:C * b + C].indirect(T.mw[:]), T.mb[:, C * b:C * b + C], O.add, ["rb%d" % b, "mw", "mb%d" % b], ["xt%d" % b], GATHER)
-            added([2, 3])
-            op("y", lambda: g.sync.dma_start(T.oc[:], T.tq[:].bitcast(dt.uint8)), ["tq"], [], "st_occ", 16, lat=2.5)
-            for a in range(4):
-                op("y", lambda a=a: g.sync.dma_start(T.osc[4 * a:4 * a + 4, :], T.tp[32 * a:32 * a + 4, :]), ["tp"], [], "st_oss", 16, lat=2.5)
             mm(4, "vq", "vp", 0, "tq", "tp")
-            act(T.yo[:], bank(4), AF.Copy, [], ["ps4", "yo"], cost=PLAIN)
-            op("y", lambda: g.sync.dma_start(T.y[:], T.yo[:]), ["yo"], [], "st_oy", 16, lat=2.5)
-    for n, e in ordered():
+            store("y", "occ", T.oc[:], T.tq[:].bitcast(dt.uint8), ["tq"])
+            for a in range(4): store("y" if a < 2 else "s", "oss", T.osc[4 * a:4 * a + 4, :], T.tp[32 * a:32 * a + 4, :], ["tp"])
+            cp(T.yo[:], bank(4), [], ["ps4", "yo"], PLAIN)
+            store("y", "oy", T.y[:], T.yo[:], ["yo"])
+    for n, e, t in ordered():
         if n["send"]: n["send"]()
         else: issue(n, e)
     settle("g", set(count.items()))
+
+
+YIELD = 0.3
+EARLY = 20.0
+EAGER = {"aw", "eq0", "eq1", "eq2", "eq3", "low", "hiw", "cq", "vq", "vo"}

@@ -3,14 +3,16 @@ from concourse.mybir import dt, AluOpType as O, ActivationFunctionType as AF
 C = 288
 K = C // 16
 STEPS = [1, 2, 4]
-RADIX = [3, 3, 4, 4]
-UNIT = 146
-LEN = 145
-TOP = UNIT * C
-TINY, PLAIN, HALF, BOTH, GATHER, SCATTER, NEAR, WAKE, SLACK, FLIGHT, HOP = 0.082, 0.31, 0.2, 0.6, 0.488, 1.04, 0.064, 0.191, 0.094, 5.5, 2.5
+JUMPS = [0, 1, 2, 3, 4, 5, 6, 4]
+PIECES = [(0, 8), (8, 18)]
+LEN = 145 * C
+TOP = 146 * C
 MID = 144
 HOLD, DROP = float(2 ** 19), float(-2 ** 21)
 FUSED, TURNED = (0, 1), (2, 3)
+TINY, PLAIN, HALF, GATHER, SCATTER, NEAR, WAKE, FLIGHT, HOP = 0.082, 0.31, 0.2, 0.488, 1.04, 0.064, 0.191, 7.0, 2.5
+SLACK, YIELD = 0.07, 1.5
+EAGER = {"xw0": 4.0, "xw1": 4.0, "yw": 2.0, "rb3": 8.0, "rb1": 0.5}
 
 F32, BF, F16, I32, U16, U8, MX = "float32", "bfloat16", "float16", "int32", "uint16", "uint8", "float8_e4m3fn_x4"
 
@@ -26,21 +28,21 @@ SCRATCH = {
     "vq": sb(128, MX), "vp": sb(128, U8), "eq": sb(512, MX), "ep": sb(512, U8),
     "tq": sb(C, MX), "tp": sb(C, U8), "zq": sb(C, MX), "zp": sb(C, U8),
     "et": sb(516, BF), "one": sb(516, BF), "zt": sb(4 * C, BF),
-    "di": sb(K, I32), "dm": sb(K, I32), "ka": sb(K, F32), "kb": sb(K, F32), "kc": sb(16, F32), "kd": sb(16, F32), "iw": sb(K, U16), "cu": sb(K, F32),
-    "cf": sb(C, F32), "ku": sb(C, F32), "kr": sb(C, F32), "hc": sb(C, F32), "hh": sb(C, BF), "cn1": sb(1, F32),
-    "pp": sb(1, I32), "pm": sb(1, I32), "pf": sb(1, F32), "cor": sb(1, F32), "coh": sb(1, F32), "con": sb(1, F32), "cn0": sb(1, F32),
-    "c72": sb(1, F32), "c73": sb(1, F32), "cln": sb(1, F32), "co2": sb(1, F32), "cov": sb(1, F32), "ctp": sb(1, F32),
-    "cw0": sb(K, F32), "cw": sb(K, F32), "kst": sb(K, F32), "kx": sb(K, F32), "kx2": sb(K, F32), "ou0": sb(8, I32), "ou": sb(8, U16),
-    "pw": sb(K, U16), "qw": sb(K, U16), "low": sb(K, U16), "hiw": sb(K, U16), "dmw": sb(K, F32), "muf": sb(K, F32), "cq": sb(K, F32),
-    "qa": sb(C, F32), "qb": sb(C, F32), "arl": sb(C, F32), "aab": sb(C, F32), "aw": sb(K, U16),
-    "ex": sb(C, F32), "ex1": sb(C, F32), "exa": sb(C, F32), "eh": sb(C, F16),
-    "nf": sb(C, BF), "ss": sb(C, F32), "v0": sb(C, F32), "v1": sb(C, F32), "v2": sb(C, F32), "bw": sb(K, U16),
+    "di": sb(K, I32), "dm": sb(K, I32), "ka": sb(K, F32), "kb": sb(K, F32), "kc": sb(16, F32), "iw": sb(K, U16),
+    "cf": sb(C, F32), "hc": sb(C, F32), "hh": sb(C, BF),
+    "pp": sb(1, I32), "pm": sb(1, I32), "pf": sb(1, F32), "cor": sb(1, F32), "coh": sb(1, F32),
+    "cmd": sb(1, F32), "co2": sb(1, F32), "cov": sb(1, F32), "ctp": sb(1, F32),
+    "cw0": sb(K, F32), "cw": sb(K, F32), "kx": sb(K, F32), "kx2": sb(K, F32), "ou0": sb(8, I32), "ou": sb(8, U16),
+    "pw": sb(K, U16), "qw": sb(K, U16), "mu": sb(K, U16), "mp": sb(K, F32), "low": sb(K, U16), "hiw": sb(K, U16),
+    "dmw": sb(K, F32), "muf": sb(K, F32), "cq": sb(K, F32), "qa": sb(C, BF), "aab": sb(C, F32),
+    "ex": sb(C, F32), "ex1": sb(C, F32), "eh": sb(C, F16), "ei": sb(C, F16),
+    "nf": sb(C, F32), "ss": sb(C, F32), "v0": sb(C, F32), "v1": sb(C, F32), "v2": sb(C, F32),
     "vx": sb(2 * C, F32), "val": sb(C, F32), "tab": sb(TOP + C, F32), "gj": sb(C, F32),
-    "sf": sb(K, F32), "xs": sb(K, F32), "mx": sb(K, F32), "vo": sb(K, U16), "si": sb(K, I32), "xr": sb(K, F32),
-    "pg": sb(2 * K, F32), "po": sb(2 * K, U16), "f1": sb(K, F32), "f2": sb(K, F32), "fo": sb(K, U16),
+    "sf": sb(K, F32), "xs": sb(K, F32), "mx": sb(K, F32), "vo": sb(K, U16), "si": sb(K, I32), "sn": sb(K, F32), "xr": sb(K, F32),
+    "pg": sb(2 * K, F32), "po": sb(2 * K, U16), "gx": sb(K, F32), "f2": sb(K, F32), "fo": sb(K, U16),
     "mf": sb(C, BF), "mw": sb(K, U16),
     "st": sb(C, F32), "su": sb(C, F32), "sg": sb(C, BF), "zm": sb(K, F32), "of": sb(K, F32),
-    "sw": sb(K, U16), "sx": sb(C, F32), "yf": sb(C, BF), "yw": sb(K, U16),
+    "sw": sb(K, U16), "sp": sb(C, BF), "sx": sb(C, BF), "yf": sb(C, BF), "yw": sb(K, U16),
     "hb": sb(4 * C, BF), "ga": sb(4 * C, BF), "fa": sb(4 * C, BF), "fm": sb(4 * C, BF), "rb": sb(4 * C, F32), "yo": sb(C, F32),
     "ps": ("psum", [128, 4096], F32),
 }
@@ -49,6 +51,9 @@ for _k in range(3):
     SCRATCH["rp%d" % _k] = sb(C, U8)
     SCRATCH["ra%d" % _k] = sb(K, U16)
     SCRATCH["rm%d" % _k] = sb(K, U16)
+for _k in range(7):
+    SCRATCH["xf%d" % _k] = sb(C, BF)
+    SCRATCH["xw%d" % _k] = sb(K, U16)
 LOADS = ["pi", "qi", "mi", "xt", "ut", "vt", "wq", "wp"]
 STORES = ["oy", "oq", "occ", "oss"]
 SEMAPHORES = ["v", "s", "t", "g"] + ["ld_" + a for a in LOADS] + ["st_" + a for a in STORES] + [a + b + str(k) for a in ("in", "out") for b in "qam" for k in range(3)]
@@ -132,7 +137,7 @@ def rank_program(g, core, T, topo):
             for j in p: succ[j].append(i)
         rank_ = [0.0] * len(nodes)
         for i in range(len(nodes) - 1, -1, -1):
-            rank_[i] = (EARLY if EAGER & set(nodes[i]["wr"]) else 0.0) + nodes[i]["cost"] + nodes[i]["lat"] + max([rank_[j] + (NEAR if nodes[j]["e"] == nodes[i]["e"] else WAKE) for j in succ[i]] + [0.0])
+            rank_[i] = max([EAGER.get(a, 0.0) for a in nodes[i]["wr"]] + [0.0]) + nodes[i]["cost"] + nodes[i]["lat"] + max([rank_[j] + (NEAR if nodes[j]["e"] == nodes[i]["e"] else WAKE) for j in succ[i]] + [0.0])
         free, end, todo = {e: 0.0 for e in queue}, {}, [len(p) for p in preds]
         ready, open_, out = {}, [i for i in range(len(nodes)) if not preds[i]], []
         for i in open_: ready[i] = 0.0
@@ -157,20 +162,16 @@ def rank_program(g, core, T, topo):
                     ready[j] = max([end[a] + (NEAR if nodes[a]["e"] == nodes[j]["e"] else WAKE) for a in preds[j]])
         return out
 
-    def held(name, key, out):
-        scan(T[out][:], T.hc[:], name, 0.0, O.add, O.max, ["hc", key], [out])
+    def held(a, keys, out):
+        scan(T[out][:], T.hc[:], a, 0.0, O.add, O.max, ["hc"] + keys, [out])
         return T[out][:, 15:C:16]
 
-    def short(name):
-        scan(T.eh[:], T.hh[:], T[name][:], 0.0, O.add, O.max, ["hh", name], ["eh"], HALF)
-        return T.eh[:, 15:C:16]
+    def short(name, e="eh"):
+        scan(T[e][:], T.hh[:], T[name][:], 0.0, O.add, O.max, ["hh", name], [e], HALF)
+        return T[e][:, 15:C:16]
 
-    def unwrap(name, w):
-        ts(T[w][:], short(name), T.coh[:, 0:1], None, O.subtract, None, ["eh", "coh"], [w])
-
-    def pointers(name, w, out):
-        scan(T[out][:], T[name][:], T.kr[:], DROP, O.max, O.add, ["kr", name], [out])
-        ts(T[w][:], T[out][:, 15:C:16], T.c72[:, 0:1], 1.0 / UNIT, O.subtract, O.mult, [out, "c72"], [w])
+    def unwrap(name, w, e="eh"):
+        ts(T[w][:], short(name, e), T.coh[:, 0:1], None, O.subtract, None, [e, "coh"], [w])
 
     def bank(b, n=C):
         return T.ps[:, 512 * b:512 * b + n]
@@ -206,6 +207,9 @@ def rank_program(g, core, T, topo):
     def part(name, b):
         return T[name][:, C * b:C * b + C]
 
+    def share(cost, fixed, a, z):
+        return fixed + (cost - fixed) * (z - a) / K
+
     load("y", "qi", T.qi[:], T.ql[:])
     load("s", "xt", T.xt[:], T.x[:])
     load("y", "ut", T.ut[:], T.u[:])
@@ -226,45 +230,43 @@ def rank_program(g, core, T, topo):
     ts(T.ka[:], T.dm[:], 1.0, DROP, O.is_equal, O.mult, ["dm"], ["ka"])
     ts(T.kb[:], T.dm[:], 2.0, HOLD, O.is_equal, O.mult, ["dm"], ["kb"])
     tt(T.kc[:], T.ka[:, 0:16], T.kb[:, 0:16], O.add, ["ka", "kb"], ["kc"])
-    tt(T.kd[:], T.ka[:, 1:17], T.kb[:, 1:17], O.add, ["ka", "kb"], ["kd"])
     ts(T.pm[:], T.pp[:], 15, None, O.bitwise_and, None, ["pp"], ["pm"])
     cp(T.pf[:], T.pm[:], ["pm"], ["pf"])
     ts(T.iw[:], T.cw0[:], 0.0, T.pf[:, 0:1], O.mult, O.add, ["cw0", "pf"], ["iw"])
-    act(T.kr[:], T.kd[:].indirect(T.iw[:]), ["kd", "iw"], ["kr"])
-    act(T.cu[:], T.cw0[:], ["cw0"], ["cu"], TINY, scale=float(UNIT))
-    tt(T.kr[:, 15:C:16], T.kr[:, 15:C:16], T.cu[:], O.add, ["cu"], ["kr"])
-    act(T.hc[:], T.kc[:].indirect(T.iw[:]), ["kc", "iw"], ["hc"])
-    act(T.hh[:], T.hc[:], ["hc"], ["hh"], PLAIN, scale=2.0 ** -10)
-    act(T.ku[:], T.cf[:], ["cf"], ["ku"], PLAIN, scale=-float(UNIT), bias=1.0)
+    act(T.hh[:], T.kc[:].indirect(T.iw[:]), ["kc", "iw"], ["hh"], scale=2.0 ** -10)
+    act(T.hc[:], T.hh[:], ["hh"], ["hc"], PLAIN, scale=2.0 ** 10)
     act(T.vx[:, 0:C], T.cf[:], ["cf"], ["vc"], PLAIN, bias=float(TOP + LEN))
     act(T.tab[:, TOP:TOP + C], T.cf[:], ["cf"], ["tc"], PLAIN, bias=float(TOP + LEN))
     ts(T.cor[:], T.pf[:], 15.0, HOLD, O.is_lt, O.mult, ["pf"], ["cor"])
-    ts(T.cn0[:], T.pf[:], 0.0, DROP, O.is_equal, O.mult, ["pf"], ["cn0"])
-    act(T.cn1[:], T.pf[:], ["pf", "cn0"], ["cn1"], TINY, scale=-float(UNIT), bias=T.cn0[:, 0:1])
-    for name, of, scale, bias in (("con", "cn1", 1.0, HOLD), ("c72", "cn1", 1.0, HOLD + 72), ("c73", "cor", 1.0, 73), ("cln", "cor", 1.0, LEN), ("co2", "cor", 2.0, LEN),
-                                  ("cov", "cor", 2.0, LEN + TOP - C), ("ctp", "cor", 2.0, LEN + TOP), ("coh", "cor", 2.0 ** -10, -MID)):
-        act(T[name][:], T[of][:], [of], [name], TINY, scale=scale, bias=float(bias))
+    for name, scale, bias in (("cmd", 1.0, (C - 1) / 2), ("co2", 2.0, LEN), ("cov", 1.0, LEN + TOP - C), ("ctp", 1.0, LEN + TOP), ("coh", 2.0 ** -10, -MID)):
+        act(T[name][:], T.cor[:], ["cor"], [name], TINY, scale=scale, bias=float(bias))
     act(T.cw[:], T.cw0[:], ["cw0", "pf"], ["cw"], TINY, bias=T.pf[:, 0:1])
-    act(T.kst[:], T.cw[:], ["cw", "con"], ["kst"], TINY, scale=float(UNIT), bias=T.con[:, 0:1])
     act(T.kx[:], T.cw[:], ["cw", "ctp"], ["kx"], TINY, bias=T.ctp[:, 0:1])
     act(T.kx2[:], T.cw[:], ["cw", "cov"], ["kx2"], TINY, bias=T.cov[:, 0:1])
     cp(T.ou[:], T.ou0[:], ["ou0"], ["ou"])
 
     cp(T.qw[:], T.qi[:], ["qi"], ["qw"])
     cp(T.pw[:], T.pi[:], ["pi"], ["pw"])
-    act(T.qa[:], T.cf[:].indirect(T.qw[:]), ["cf", "qw"], ["qa"], scale=float(UNIT))
-    tt(T.dmw[:], T.mi[:], T.cw[:], O.subtract, ["mi", "cw"], ["dmw"])
+    act(T.qa[:], T.cf[:].indirect(T.qw[:]), ["cf", "qw"], ["qa"], bias=-float(MID))
+    act(T.xf0[:], T.qa[:].indirect(T.pw[:]), ["qa", "pw"], ["xf0"])
+    cp(T.mu[:], T.mi[:], ["mi"], ["mu"])
+    act(T.sx[:], T.cf[:].indirect(T.mu[:]), ["cf", "mu"], ["sx"], bias=-float(MID))
+    act(T.yf[:], T.sx[:].indirect(T.pw[:]), ["sx", "pw"], ["yf"])
+    unwrap("yf", "mp")
+    tt(T.dmw[:], T.mp[:], T.pi[:], O.subtract, ["mp", "pi"], ["dmw"])
     ts(T.muf[:], T.dmw[:], T.cor[:, 0:1], 2.0 ** -10, O.mult, O.mult, ["dmw", "cor"], ["muf"])
-    tt(T.cq[:], T.cw[:], T.muf[:], O.subtract, ["cw", "muf"], ["cq"])
-    for w, o in (("low", O.min), ("hiw", O.max)):
-        tt(T.muf[:], T.mi[:], T.cw[:], o, ["mi", "cw"], ["muf"])
-        cp(T[w][:], T.muf[:], ["muf"], [w])
+    tt(T.cq[:], T.pi[:], T.muf[:], O.subtract, ["pi", "muf"], ["cq"])
+    for w, o, a in (("low", O.min, "zm"), ("hiw", O.max, "of")):
+        tt(T[a][:], T.mp[:], T.pi[:], o, ["mp", "pi"], [a])
+        cp(T[w][:], T[a][:], [a], [w])
 
-    def ahead(k, q):
-        tt(T.arl[:], T[q][:].indirect(T.pw[:]), T.ku[:], O.add, [q, "pw", "ku"], ["arl"], GATHER)
-        act(T.aab[:], T[q][:].indirect(T.pw[:]), [q, "pw"], ["aab"], bias=1.0)
-        pointers("arl", "aw", "exa")
-        send(k, "a", [("aw", T.aw[:], "ra%d" % k, T["ra%d" % k][:])], HOP)
+    def ahead(k):
+        unwrap("xf0", "xw0", "ei")
+        send(k, "a", [("xw0", T.xw0[:], "ra%d" % k, T["ra%d" % k][:])], HOP)
+        act(T.aab[:], T.xf0[:], ["xf0"], ["aab"], PLAIN, bias=float(MID + C * (1 + sum(2 ** n for n in JUMPS))))
+        for n in range(max(JUMPS)):
+            act(T["xf%d" % (n + 1)][:], T["xf%d" % n][:].indirect(T["xw%d" % n][:]), ["xf%d" % n, "xw%d" % n], ["xf%d" % (n + 1)])
+            unwrap("xf%d" % (n + 1), "xw%d" % (n + 1), "ei")
 
     def state(k):
         mm(4, "ur", "urp", 0, "tq", "tp")
@@ -279,64 +281,66 @@ def rank_program(g, core, T, topo):
         op("v", lambda b=b: V.quantize_mx(T.eq[:, 128 * b:128 * b + 128], T.ep[:, 128 * b:128 * b + 128], T.et[:, 3 - b:515 - b]), ["et"], ["eq%d" % b], cost=0.15)
     quant("vq", "vp", "vt", 128)
     state(0)
-    ahead(0, "qa")
+    ahead(0)
 
-    qcur = ["qa", "qb"]
     for k in range(len(STEPS)):
         final = k == len(STEPS) - 1
-        ts(T.nf[:], bank(4), 0.0, None, O.is_ge, None, [], ["ps4", "nf"], PLAIN)
+        ts(T.nf[:], bank(4), 0.0, float(LEN - C), O.is_ge, O.mult, [], ["ps4", "nf"], PLAIN)
         act(T.ss[:], bank(4), [], ["ps4", "ss"], PLAIN)
-        tt(T.v0[:], T.nf[:], T.arl[:], O.mult, ["nf", "arl"], ["v0"], BOTH)
-        for b in range(4): act(part("fa", b), bank(b), [], ["ps%d" % b, "fa%d" % b], PLAIN, scale=32.0 if b in TURNED else 1.0)
+        for h, (a, z) in enumerate(PIECES):
+            tt(T.v0[:, 16 * a:16 * z], T.nf[:].indirect(T.xw0[:, a:z]), T.aab[:, 16 * a:16 * z], O.add, ["nf", "xw0", "aab"], ["v0%d" % h], share(GATHER, 0.05, a, z))
+        base = "v0"
+        for j, n in enumerate(JUMPS):
+            nxt = "vx" if j == len(JUMPS) - 1 else "v1" if base == "v0" else "v0"
+            at = C if nxt == "vx" else 0
+            for h, (a, z) in enumerate(PIECES):
+                act(T.v2[:, 16 * a:16 * z], T[base][:, 16 * a:16 * z], [base + str(h)], ["v2%d" % h], share(PLAIN, 0.03, a, z), bias=-float(C * 2 ** n))
+            for h, (a, z) in enumerate(PIECES):
+                tt(T[nxt][:, at + 16 * a:at + 16 * z], T[base][:].indirect(T["xw%d" % n][:, a:z]), T.v2[:, 16 * a:16 * z], O.min,
+                   [base + "0", base + "1", "v2%d" % h, "xw%d" % n], [nxt + str(h)], share(GATHER, 0.05, a, z))
+            base = nxt
+        for b in range(4): act(part("fa", b), bank(b), ["vx1"], ["ps%d" % b, "fa%d" % b], PLAIN, scale=32.0 if b in TURNED else 1.0)
         for b, at in enumerate((5, 6, 7, 4)):
             mm(at, "eq", "ep", 128 * b, "rq%d" % k, "rp%d" % k, "eq%d" % b)
-            act(part("hb", b), bank(at), [], ["ps%d" % at, "hb%d" % b], PLAIN, scale=0.5)
+            act(part("hb", b), bank(at), ["vx1"], ["ps%d" % at, "hb%d" % b], PLAIN, scale=0.5)
             act(T.ga[:, b:4 * C:4], part("hb", b).indirect(T["ra%d" % k][:]), ["hb%d" % b, "ra%d" % k], ["ga%d" % b])
-        base = "v0"
-        for n, r in enumerate(RADIX):
-            pointers(base, "bw", "ex" if n else "ex1")
-            act(T.v2[:], T[base][:], [base], ["v2"], PLAIN)
-            for j in range(r - 1):
-                nxt = "v1" if base == "v0" else "v0"
-                tt(T[nxt][:], T[base][:].indirect(T.bw[:]), T.v2[:], O.add, [base, "v2", "bw"], [nxt], GATHER)
-                base = nxt
-        tt(T.vx[:, C:2 * C], T[base][:].indirect(T.aw[:]), T.aab[:], O.add, [base, "aw", "aab"], ["vx"], GATHER)
-        tt(T.sf[:], T.ex1[:, 15:C:16], T.kst[:], O.is_equal, ["ex1", "kst"], ["sf"])
+        ts(T.sf[:], held(T.nf[:], ["nf"], "ex1"), T.cor[:, 0:1], None, O.is_equal, None, ["ex1", "cor"], ["sf"])
         tt(T.xs[:], T.sf[:], T.kx[:], O.mult, ["sf", "kx"], ["xs"])
         tt(T.mx[:], T.xs[:], T.kx2[:], O.max, ["xs", "kx2"], ["mx"])
         ts(T.vo[:], T.mx[:], T.cov[:, 0:1], None, O.subtract, None, ["mx", "cov"], ["vo"])
-        act(T.val[:], T.vx[:].indirect(T.vo[:]), ["vx", "vc", "vo"], ["val"])
-        a = held(T.vx[:, C:2 * C], "vx", "ex")
-        ts(T.si[:], a, T.c73[:, 0:1], 1.0 / UNIT, O.subtract, O.mult, ["ex", "c73"], ["si"])
+        act(T.val[:], T.vx[:].indirect(T.vo[:]), ["vx0", "vx1", "vc", "vo"], ["val"])
+        a = held(T.vx[:, C:2 * C], ["vx0", "vx1"], "ex")
+        ts(T.si[:], a, T.cmd[:, 0:1], 1.0 / C, O.subtract, O.mult, ["ex", "cmd"], ["si"])
         tt(T.xr[:], a, T.xs[:], O.add, ["ex", "xs"], ["xr"])
-        ts(T.pg[:, K:2 * K], T.si[:], float(UNIT), T.cln[:, 0:1], O.mult, O.add, ["si", "cln"], ["pgb"])
+        ts(T.sn[:], T.si[:], -float(C), float(LEN), O.mult, O.add, ["si"], ["sn"])
+        tt(T.pg[:, K:2 * K], a, T.sn[:], O.add, ["ex", "sn"], ["pgb"])
         tt(T.pg[:, 0:K], T.pg[:, K:2 * K], T.xr[:], O.min, ["pgb", "xr"], ["pga"])
+        tt(T.gx[:], T.pg[:, K:2 * K], T.xs[:], O.max, ["pgb", "xs"], ["gx"])
         ts(T.po[:], T.pg[:], T.cor[:, 0:1], None, O.subtract, None, ["pga", "pgb", "cor"], ["po"])
-        cp(T.tab[:].indirect(T.po[:, 0:K]), T.val[:], ["po", "val", "tc"], ["tab"], SCATTER)
-        tt(T.gj[:], T.tab[:].indirect(T.po[:, K:2 * K]), T.vx[:, C:2 * C], O.subtract, ["tab", "po", "vx"], ["gj"], GATHER)
-        a = held(T.gj[:], "gj", "ex")
-        tt(T.f1[:], a, T.pg[:, K:2 * K], O.add, ["ex", "pgb"], ["f1"])
-        tt(T.f2[:], T.f1[:], T.xs[:], O.max, ["f1", "xs"], ["f2"])
+        cp(T.tab[:].indirect(T.po[:, 0:K]), T.val[:], ["po", "val", "tc", "gx"], ["tab"], SCATTER)
+        tt(T.gj[:], T.tab[:].indirect(T.po[:, K:2 * K]), T.vx[:, C:2 * C], O.subtract, ["tab", "po", "vx0", "vx1"], ["gj"], GATHER)
+        tt(T.f2[:], held(T.gj[:], ["gj"], "ex"), T.gx[:], O.add, ["ex", "gx"], ["f2"])
         ts(T.fo[:], T.f2[:], T.co2[:, 0:1], None, O.subtract, None, ["f2", "co2"], ["fo"])
         ts(T.mf[:], T.tab[:].indirect(T.fo[:]), float(TOP + LEN + MID), None, O.subtract, None, ["tab", "fo"], ["mf"], GATHER)
         unwrap("mf", "mw")
         send(k, "m", [("mw", T.mw[:], "rm%d" % k, T["rm%d" % k][:])], HOP)
-        act(T.st[:], T.ss[:].indirect(T.mw[:]), ["ss", "mw"], ["st"])
-        act(T.su[:], T.st[:].indirect(T.low[:]), ["st", "low"], ["su"])
+        cp(T.st[:], T.ss[:].indirect(T.mw[:]), ["ss", "mw"], ["st"], GATHER)
+        cp(T.su[:], T.st[:].indirect(T.low[:]), ["st", "low"], ["su"], GATHER)
         tt(T.sg[:], T.st[:].indirect(T.hiw[:]), T.su[:], O.is_lt, ["st", "hiw", "su"], ["sg"], GATHER)
         tt(T.zm[:], short("sg"), T.dmw[:], O.mult, ["eh", "dmw"], ["zm"])
         tt(T.of[:], T.zm[:], T.cq[:], O.add, ["zm", "cq"], ["of"])
         cp(T.sw[:], T.of[:], ["of"], ["sw"])
-        qo, qn = qcur[k % 2], qcur[1 - k % 2]
-        act(T.yf[:], T[qo][:].indirect(T.sw[:]), [qo, "sw"], ["yf"], scale=1.0 / UNIT, bias=-float(MID))
-        act(T.sx[:], T.cf[:].indirect(T.sw[:]), ["cf", "sw"], ["sx"])
+        cp(T.yf[:], T.qa[:].indirect(T.sw[:]), ["qa", "sw"], ["yf"], GATHER)
+        act(T.sp[:], T.cf[:].indirect(T.sw[:]), ["cf", "sw"], ["sp"], bias=-float(MID))
+        act(T.sx[:], T.sp[:].indirect(T.pw[:]), ["sp", "pw"], ["sx"])
         unwrap("yf", "yw")
+        act(T.xf0[:], T.sx[:].indirect(T.yw[:]), ["sx", "yw"], ["xf0"])
         if final:
-            act(T[qn][:], T.sx[:].indirect(T.yw[:]), ["sx", "yw"], [qn])
-            store("y", "oq", T.qo[:], T[qn][0:128:16, :], [qn])
+            act(T.su[:], T.xf0[:].indirect(T.pw[:]), ["xf0", "pw"], ["su"], bias=float(MID))
+            store("y", "oq", T.qo[:], T.su[0:128:16, :], ["su"])
         else:
-            act(T[qn][:], T.sx[:].indirect(T.yw[:]), ["sx", "yw"], [qn], scale=float(UNIT))
-            ahead(k + 1, qn)
+            act(T.qa[:], T.xf0[:].indirect(T.pw[:]), ["xf0", "pw"], ["qa"])
+            ahead(k + 1)
         for b in range(4):
             tt(T.zt[:, b:4 * C:4], part("hb", b).indirect(T["rm%d" % k][:]), T.ga[:, b:4 * C:4], O.add, ["hb%d" % b, "rm%d" % k, "ga%d" % b], ["zt%d" % b], GATHER)
         quant("zq", "zp", "zt", C, ["zt0", "zt1", "zt2", "zt3"])
@@ -361,8 +365,3 @@ def rank_program(g, core, T, topo):
         if n["send"]: n["send"]()
         else: issue(n, e)
     settle("g", set(count.items()))
-
-
-YIELD = 0.3
-EARLY = 20.0
-EAGER = {"aw", "eq0", "eq1", "eq2", "eq3", "low", "hiw", "cq", "vq", "vo"}

@@ -3,16 +3,18 @@ from concourse.mybir import dt, AluOpType as O, ActivationFunctionType as AF
 C = 288
 K = C // 16
 STEPS = [1, 2, 4]
-JUMPS = [0, 1, 2, 3, 4, 5, 6, 4]
+RADIX = [2, 2, 2, 3, 2, 3]
+SEEN = 144
 PIECES = [(0, 8), (8, 18)]
 LEN = 145 * C
 TOP = 146 * C
 MID = 144
 HOLD, DROP = float(2 ** 19), float(-2 ** 21)
 FUSED, TURNED = (0, 1), (2, 3)
-TINY, PLAIN, HALF, GATHER, SCATTER, NEAR, WAKE, FLIGHT, HOP = 0.082, 0.31, 0.2, 0.488, 1.04, 0.064, 0.191, 7.0, 2.5
-SLACK, YIELD = 0.07, 1.5
-EAGER = {"xw0": 4.0, "xw1": 4.0, "yw": 2.0, "rb3": 8.0, "rb1": 0.5}
+TINY, PLAIN, HALF, GATHER, SCATTER, NEAR, WAKE, FLIGHT, HOP = 0.082, 0.31, 0.2, 0.488, 1.04, 0.064, 0.191, 7.0, 3.0
+SLACK, YIELD = 0.094, 0.3
+EAGER = {"rb00": 4, "rb10": 2, "rb11": 8, "rb30": 0.5, "zq0": 4, "zq1": 0.25, "zt00": 0.5, "xt1": 0.25, "xt2": 1, "xt3": 2, "tp": 1,
+         "xf1": 1, "xf3": 2, "xw1": 0.5, "xw3": 0.25, "xw4": 0.5, "nb": 4, "vo": 1, "mp": 4, "sw": 4}
 
 F32, BF, F16, I32, U16, U8, MX = "float32", "bfloat16", "float16", "int32", "uint16", "uint8", "float8_e4m3fn_x4"
 
@@ -35,10 +37,10 @@ SCRATCH = {
     "cw0": sb(K, F32), "cw": sb(K, F32), "kx": sb(K, F32), "kx2": sb(K, F32), "ou0": sb(8, I32), "ou": sb(8, U16),
     "pw": sb(K, U16), "qw": sb(K, U16), "mu": sb(K, U16), "mp": sb(K, F32), "low": sb(K, U16), "hiw": sb(K, U16),
     "dmw": sb(K, F32), "muf": sb(K, F32), "cq": sb(K, F32), "qa": sb(C, BF), "aab": sb(C, F32),
-    "ex": sb(C, F32), "ex1": sb(C, F32), "eh": sb(C, F16), "ei": sb(C, F16),
-    "nf": sb(C, F32), "ss": sb(C, F32), "v0": sb(C, F32), "v1": sb(C, F32), "v2": sb(C, F32),
+    "ex": sb(C, F32), "eh": sb(C, F16), "ei": sb(C, F16), "xg0": sb(C, BF), "cos": sb(1, F32),
+    "nf": sb(C, F32), "nb": sb(C, BF), "ss": sb(C, F32), "v0": sb(C, F32), "v1": sb(C, F32), "w0": sb(C, F32), "w1": sb(C, F32),
     "vx": sb(2 * C, F32), "val": sb(C, F32), "tab": sb(TOP + C, F32), "gj": sb(C, F32),
-    "sf": sb(K, F32), "xs": sb(K, F32), "mx": sb(K, F32), "vo": sb(K, U16), "si": sb(K, I32), "sn": sb(K, F32), "xr": sb(K, F32),
+    "sf": sb(K, F32), "xs": sb(K, F32), "vo": sb(K, U16), "si": sb(K, I32), "sn": sb(K, F32), "xr": sb(K, F32),
     "pg": sb(2 * K, F32), "po": sb(2 * K, U16), "gx": sb(K, F32), "f2": sb(K, F32), "fo": sb(K, U16),
     "mf": sb(C, BF), "mw": sb(K, U16),
     "st": sb(C, F32), "su": sb(C, F32), "sg": sb(C, BF), "zm": sb(K, F32), "of": sb(K, F32),
@@ -51,7 +53,7 @@ for _k in range(3):
     SCRATCH["rp%d" % _k] = sb(C, U8)
     SCRATCH["ra%d" % _k] = sb(K, U16)
     SCRATCH["rm%d" % _k] = sb(K, U16)
-for _k in range(7):
+for _k in range(len(RADIX)):
     SCRATCH["xf%d" % _k] = sb(C, BF)
     SCRATCH["xw%d" % _k] = sb(K, U16)
 LOADS = ["pi", "qi", "mi", "xt", "ut", "vt", "wq", "wp"]
@@ -204,16 +206,16 @@ def rank_program(g, core, T, topo):
 
         op("g", None, [a for a, x, b, y in pairs], [b for a, x, b, y in pairs], cost=0.3 * len(pairs), lat=lat, send=go)
 
-    def part(name, b):
-        return T[name][:, C * b:C * b + C]
+    def part(name, b, a=0, z=K):
+        return T[name][:, C * b + 16 * a:C * b + 16 * z]
 
     def share(cost, fixed, a, z):
         return fixed + (cost - fixed) * (z - a) / K
 
     load("y", "qi", T.qi[:], T.ql[:])
     load("s", "xt", T.xt[:], T.x[:])
-    load("y", "ut", T.ut[:], T.u[:])
     load("y", "pi", T.pi[:], T.pl[:])
+    load("s", "ut", T.ut[:], T.u[:])
     load("y", "mi", T.mi[:], T.ml[:])
     load("y", "wq", T.wq[:].bitcast(dt.uint8), T.wc[:])
     load("y", "wp", T.wp[:], T.ws[:])
@@ -238,7 +240,7 @@ def rank_program(g, core, T, topo):
     act(T.vx[:, 0:C], T.cf[:], ["cf"], ["vc"], PLAIN, bias=float(TOP + LEN))
     act(T.tab[:, TOP:TOP + C], T.cf[:], ["cf"], ["tc"], PLAIN, bias=float(TOP + LEN))
     ts(T.cor[:], T.pf[:], 15.0, HOLD, O.is_lt, O.mult, ["pf"], ["cor"])
-    for name, scale, bias in (("cmd", 1.0, (C - 1) / 2), ("co2", 2.0, LEN), ("cov", 1.0, LEN + TOP - C), ("ctp", 1.0, LEN + TOP), ("coh", 2.0 ** -10, -MID)):
+    for name, scale, bias in (("cmd", 1.0, (C - 1) / 2), ("co2", 2.0, LEN), ("cov", 1.0, LEN + TOP - C), ("ctp", 1.0, LEN + TOP), ("coh", 2.0 ** -10, -MID), ("cos", 2.0 ** -10, 0)):
         act(T[name][:], T.cor[:], ["cor"], [name], TINY, scale=scale, bias=float(bias))
     act(T.cw[:], T.cw0[:], ["cw0", "pf"], ["cw"], TINY, bias=T.pf[:, 0:1])
     act(T.kx[:], T.cw[:], ["cw", "ctp"], ["kx"], TINY, bias=T.ctp[:, 0:1])
@@ -263,10 +265,14 @@ def rank_program(g, core, T, topo):
     def ahead(k):
         unwrap("xf0", "xw0", "ei")
         send(k, "a", [("xw0", T.xw0[:], "ra%d" % k, T["ra%d" % k][:])], HOP)
-        act(T.aab[:], T.xf0[:], ["xf0"], ["aab"], PLAIN, bias=float(MID + C * (1 + sum(2 ** n for n in JUMPS))))
-        for n in range(max(JUMPS)):
-            act(T["xf%d" % (n + 1)][:], T["xf%d" % n][:].indirect(T["xw%d" % n][:]), ["xf%d" % n, "xw%d" % n], ["xf%d" % (n + 1)])
-            unwrap("xf%d" % (n + 1), "xw%d" % (n + 1), "ei")
+        act(T.aab[:], T.xf0[:], ["xf0"], ["aab"], PLAIN, bias=float(MID + C * SEEN))
+        for n, r in enumerate(RADIX[:-1]):
+            cur = "xf%d" % n
+            for j in range(r - 1):
+                nxt = "xf%d" % (n + 1) if j == r - 2 else "xg%d" % j
+                act(T[nxt][:], T[cur][:].indirect(T["xw%d" % n][:]), [cur, "xw%d" % n], [nxt])
+                cur = nxt
+            unwrap(cur, "xw%d" % (n + 1), "ei")
 
     def state(k):
         mm(4, "ur", "urp", 0, "tq", "tp")
@@ -286,28 +292,32 @@ def rank_program(g, core, T, topo):
     for k in range(len(STEPS)):
         final = k == len(STEPS) - 1
         ts(T.nf[:], bank(4), 0.0, float(LEN - C), O.is_ge, O.mult, [], ["ps4", "nf"], PLAIN)
-        act(T.ss[:], bank(4), [], ["ps4", "ss"], PLAIN)
         for h, (a, z) in enumerate(PIECES):
             tt(T.v0[:, 16 * a:16 * z], T.nf[:].indirect(T.xw0[:, a:z]), T.aab[:, 16 * a:16 * z], O.add, ["nf", "xw0", "aab"], ["v0%d" % h], share(GATHER, 0.05, a, z))
-        base = "v0"
-        for j, n in enumerate(JUMPS):
-            nxt = "vx" if j == len(JUMPS) - 1 else "v1" if base == "v0" else "v0"
-            at = C if nxt == "vx" else 0
-            for h, (a, z) in enumerate(PIECES):
-                act(T.v2[:, 16 * a:16 * z], T[base][:, 16 * a:16 * z], [base + str(h)], ["v2%d" % h], share(PLAIN, 0.03, a, z), bias=-float(C * 2 ** n))
-            for h, (a, z) in enumerate(PIECES):
-                tt(T[nxt][:, at + 16 * a:at + 16 * z], T[base][:].indirect(T["xw%d" % n][:, a:z]), T.v2[:, 16 * a:16 * z], O.min,
-                   [base + "0", base + "1", "v2%d" % h, "xw%d" % n], [nxt + str(h)], share(GATHER, 0.05, a, z))
-            base = nxt
+        cur, s = "v0", 1
+        for n, r in enumerate(RADIX):
+            for j in range(r - 1):
+                for hs, (a, z) in ([("01", (0, K))] if j else zip("01", PIECES)):
+                    act(T["w%d" % j][:, 16 * a:16 * z], T[cur][:, 16 * a:16 * z], [cur + h for h in hs], ["w%d%s" % (j, h) for h in hs], share(PLAIN, 0.03, a, z), bias=-float(C * s * (j + 1)))
+            for j in range(r - 1):
+                nxt = "vx" if (n, j) == (len(RADIX) - 1, r - 2) else "v1" if cur == "v0" else "v0"
+                at = C if nxt == "vx" else 0
+                for hs, (a, z) in ([("01", (0, K))] if nxt == "vx" else zip("01", PIECES)):
+                    tt(T[nxt][:, at + 16 * a:at + 16 * z], T[cur][:].indirect(T["xw%d" % n][:, a:z]), T["w%d" % j][:, 16 * a:16 * z], O.min,
+                       [cur + "0", cur + "1", "xw%d" % n] + ["w%d%s" % (j, h) for h in hs], [nxt + h for h in hs], share(GATHER, 0.05, a, z))
+                cur = nxt
+            s *= r
+        act(T.ss[:], bank(4), ["vx1"], ["ps4", "ss"], PLAIN)
         for b in range(4): act(part("fa", b), bank(b), ["vx1"], ["ps%d" % b, "fa%d" % b], PLAIN, scale=32.0 if b in TURNED else 1.0)
         for b, at in enumerate((5, 6, 7, 4)):
             mm(at, "eq", "ep", 128 * b, "rq%d" % k, "rp%d" % k, "eq%d" % b)
             act(part("hb", b), bank(at), ["vx1"], ["ps%d" % at, "hb%d" % b], PLAIN, scale=0.5)
             act(T.ga[:, b:4 * C:4], part("hb", b).indirect(T["ra%d" % k][:]), ["hb%d" % b, "ra%d" % k], ["ga%d" % b])
-        ts(T.sf[:], held(T.nf[:], ["nf"], "ex1"), T.cor[:, 0:1], None, O.is_equal, None, ["ex1", "cor"], ["sf"])
+        act(T.nb[:], T.nf[:], ["nf"], ["nb"], PLAIN, scale=1.0 / (LEN - C))
+        ts(T.sf[:], short("nb"), T.cos[:, 0:1], None, O.is_equal, None, ["eh", "cos"], ["sf"])
         tt(T.xs[:], T.sf[:], T.kx[:], O.mult, ["sf", "kx"], ["xs"])
-        tt(T.mx[:], T.xs[:], T.kx2[:], O.max, ["xs", "kx2"], ["mx"])
-        ts(T.vo[:], T.mx[:], T.cov[:, 0:1], None, O.subtract, None, ["mx", "cov"], ["vo"])
+        tt(T.xr[:], T.xs[:], T.kx2[:], O.max, ["xs", "kx2"], ["xr"])
+        ts(T.vo[:], T.xr[:], T.cov[:, 0:1], None, O.subtract, None, ["xr", "cov"], ["vo"])
         act(T.val[:], T.vx[:].indirect(T.vo[:]), ["vx0", "vx1", "vc", "vo"], ["val"])
         a = held(T.vx[:, C:2 * C], ["vx0", "vx1"], "ex")
         ts(T.si[:], a, T.cmd[:, 0:1], 1.0 / C, O.subtract, O.mult, ["ex", "cmd"], ["si"])
@@ -324,13 +334,14 @@ def rank_program(g, core, T, topo):
         ts(T.mf[:], T.tab[:].indirect(T.fo[:]), float(TOP + LEN + MID), None, O.subtract, None, ["tab", "fo"], ["mf"], GATHER)
         unwrap("mf", "mw")
         send(k, "m", [("mw", T.mw[:], "rm%d" % k, T["rm%d" % k][:])], HOP)
-        cp(T.st[:], T.ss[:].indirect(T.mw[:]), ["ss", "mw"], ["st"], GATHER)
-        cp(T.su[:], T.st[:].indirect(T.low[:]), ["st", "low"], ["su"], GATHER)
+        pick = act if final else cp
+        pick(T.st[:], T.ss[:].indirect(T.mw[:]), ["ss", "mw"], ["st"], GATHER)
+        pick(T.su[:], T.st[:].indirect(T.low[:]), ["st", "low"], ["su"], GATHER)
         tt(T.sg[:], T.st[:].indirect(T.hiw[:]), T.su[:], O.is_lt, ["st", "hiw", "su"], ["sg"], GATHER)
         tt(T.zm[:], short("sg"), T.dmw[:], O.mult, ["eh", "dmw"], ["zm"])
         tt(T.of[:], T.zm[:], T.cq[:], O.add, ["zm", "cq"], ["of"])
         cp(T.sw[:], T.of[:], ["of"], ["sw"])
-        cp(T.yf[:], T.qa[:].indirect(T.sw[:]), ["qa", "sw"], ["yf"], GATHER)
+        pick(T.yf[:], T.qa[:].indirect(T.sw[:]), ["qa", "sw"], ["yf"], GATHER)
         act(T.sp[:], T.cf[:].indirect(T.sw[:]), ["cf", "sw"], ["sp"], bias=-float(MID))
         act(T.sx[:], T.sp[:].indirect(T.pw[:]), ["sp", "pw"], ["sx"])
         unwrap("yf", "yw")
@@ -341,17 +352,23 @@ def rank_program(g, core, T, topo):
         else:
             act(T.qa[:], T.xf0[:].indirect(T.pw[:]), ["xf0", "pw"], ["qa"])
             ahead(k + 1)
-        for b in range(4):
-            tt(T.zt[:, b:4 * C:4], part("hb", b).indirect(T["rm%d" % k][:]), T.ga[:, b:4 * C:4], O.add, ["hb%d" % b, "rm%d" % k, "ga%d" % b], ["zt%d" % b], GATHER)
-        quant("zq", "zp", "zt", C, ["zt0", "zt1", "zt2", "zt3"])
+        for h, (a, z) in enumerate(PIECES):
+            for b in range(4):
+                tt(T.zt[:, 64 * a + b:64 * z:4], part("hb", b).indirect(T["rm%d" % k][:, a:z]), T.ga[:, 64 * a + b:64 * z:4], O.add, ["hb%d" % b, "rm%d" % k, "ga%d" % b], ["zt%d%d" % (b, h)], share(GATHER, 0.05, a, z))
+            op("v", lambda a=a, z=z: V.quantize_mx(T.zq[:, 16 * a:16 * z], T.zp[:, 16 * a:16 * z], T.zt[:, 64 * a:64 * z]), ["zt%d%d" % (b, h) for b in range(4)], ["zq%d" % h], cost=share(0.32, 0.02, a, z))
+            for b in TURNED + FUSED:
+                op("t", lambda a=a, z=z, b=b, h=h: g.tensor.matmul_mx(bank(4 * h + b, 16 * (z - a)), T.wq[:, 128 * b:128 * b + 128], T.wp[:, 128 * b:128 * b + 128], T.zq[:, 16 * a:16 * z], T.zp[:, 16 * a:16 * z], True, True),
+                   ["wq", "wp", "zq%d" % h], ["ps%d" % (4 * h + b)], cost=share(0.3, 0.02, a, z))
         for b in TURNED: act(part("fm", b), part("fa", b).indirect(T.mw[:]), ["fa%d" % b, "mw"], ["fm%d" % b])
-        for b in (FUSED[0], TURNED[0], FUSED[1], TURNED[1]): mm(b, "wq", "wp", 128 * b, "zq", "zp")
+        for h, (a, z) in enumerate(PIECES):
+            for b in FUSED:
+                act(part("rb", b, a, z), bank(4 * h + b, 16 * (z - a)), [], ["ps%d" % (4 * h + b), "rb%d%d" % (b, h)], share(PLAIN, 0.03, a, z), scale=0.03125)
+            for b in TURNED:
+                tt(part("rb", b, a, z), bank(4 * h + b, 16 * (z - a)), part("fm", b, a, z), O.add, ["fm%d" % b], ["ps%d" % (4 * h + b), "rb%d%d" % (b, h)], share(PLAIN, 0.03, a, z))
         for b in FUSED:
-            act(part("rb", b), bank(b), [], ["ps%d" % b, "rb%d" % b], PLAIN, scale=0.03125)
-            tt(T.xt[:, b:4 * C:4], part("rb", b).indirect(T.mw[:]), part("fa", b), O.add, ["rb%d" % b, "mw", "fa%d" % b], ["xt%d" % b], GATHER)
+            tt(T.xt[:, b:4 * C:4], part("rb", b).indirect(T.mw[:]), part("fa", b), O.add, ["rb%d0" % b, "rb%d1" % b, "mw", "fa%d" % b], ["xt%d" % b], GATHER)
         for b in TURNED:
-            tt(part("rb", b), bank(b), part("fm", b), O.add, ["fm%d" % b], ["ps%d" % b, "rb%d" % b], PLAIN)
-            act(T.xt[:, b:4 * C:4], part("rb", b).indirect(T.mw[:]), ["rb%d" % b, "mw"], ["xt%d" % b], scale=0.03125)
+            act(T.xt[:, b:4 * C:4], part("rb", b).indirect(T.mw[:]), ["rb%d0" % b, "rb%d1" % b, "mw"], ["xt%d" % b], scale=0.03125)
         quant("tq", "tp", "xt", C, ["xt", "xt0", "xt1", "xt2", "xt3"])
         if not final:
             state(k + 1)
@@ -359,8 +376,8 @@ def rank_program(g, core, T, topo):
             mm(4, "vq", "vp", 0, "tq", "tp")
             store("y", "occ", T.oc[:], T.tq[:].bitcast(dt.uint8), ["tq"])
             for a in range(4): store("y" if a < 2 else "s", "oss", T.osc[4 * a:4 * a + 4, :], T.tp[32 * a:32 * a + 4, :], ["tp"])
-            cp(T.yo[:], bank(4), [], ["ps4", "yo"], PLAIN)
-            store("y", "oy", T.y[:], T.yo[:], ["yo"])
+            act(T.yo[:], bank(4), [], ["ps4", "yo"], PLAIN)
+            store("s", "oy", T.y[:], T.yo[:], ["yo"])
     for n, e, t in ordered():
         if n["send"]: n["send"]()
         else: issue(n, e)

from concourse.mybir import dt, AluOpType as O, ActivationFunctionType as AF

C = 288
K = C // 16
STEPS = [1, 2, 4]
RADIX = [2, 2, 2, 3, 2, 3]
SEEN = 144
PIECES = [(0, 8), (8, 18)]
LEN = 145 * C
TOP = 146 * C
MID = 144
HOLD, DROP = float(2 ** 19), float(-2 ** 21)
FUSED, TURNED = (0, 1), (2, 3)
TINY, PLAIN, HALF, GATHER, SCATTER, NEAR, WAKE, FLIGHT, HOP = 0.082, 0.31, 0.2, 0.488, 1.04, 0.064, 0.191, 7.0, 3.0
SLACK, YIELD = 0.094, 0.3
EAGER = {"rb00": 4, "rb10": 2, "rb11": 8, "rb30": 0.5, "zq0": 4, "zq1": 0.25, "zt00": 0.5, "xt1": 0.25, "xt2": 1, "xt3": 2, "tp": 1,
         "xf1": 1, "xf3": 2, "xw1": 0.5, "xw3": 0.25, "xw4": 0.5, "nb": 4, "vo": 1, "mp": 4, "sw": 4}

F32, BF, F16, I32, U16, U8, MX = "float32", "bfloat16", "float16", "int32", "uint16", "uint8", "float8_e4m3fn_x4"


def sb(n, d):
    return ("sbuf", [128, n], d)


SCRATCH = {
    "xt": sb(4 * C, BF), "ut": sb(512, BF), "vt": sb(512, BF),
    "pi": sb(K, I32), "qi": sb(K, I32), "mi": sb(K, I32),
    "wq": sb(512, MX), "wp": sb(512, U8), "uq": sb(128, MX), "up": sb(128, U8), "ur": sb(128, MX), "urp": sb(128, U8),
    "vq": sb(128, MX), "vp": sb(128, U8), "eq": sb(512, MX), "ep": sb(512, U8),
    "tq": sb(C, MX), "tp": sb(C, U8), "zq": sb(C, MX), "zp": sb(C, U8),
    "et": sb(516, BF), "one": sb(516, BF), "zt": sb(4 * C, BF),
    "di": sb(K, I32), "dm": sb(K, I32), "ka": sb(K, F32), "kb": sb(K, F32), "kc": sb(16, F32), "iw": sb(K, U16),
    "cf": sb(C, F32), "hc": sb(C, F32), "hh": sb(C, BF),
    "pp": sb(1, I32), "pm": sb(1, I32), "pf": sb(1, F32), "cor": sb(1, F32), "coh": sb(1, F32),
    "cmd": sb(1, F32), "co2": sb(1, F32), "cov": sb(1, F32), "ctp": sb(1, F32),
    "cw0": sb(K, F32), "cw": sb(K, F32), "kx": sb(K, F32), "kx2": sb(K, F32), "ou0": sb(8, I32), "ou": sb(8, U16),
    "pw": sb(K, U16), "qw": sb(K, U16), "mu": sb(K, U16), "mp": sb(K, F32), "low": sb(K, U16), "hiw": sb(K, U16),
    "dmw": sb(K, F32), "muf": sb(K, F32), "cq": sb(K, F32), "qa": sb(C, BF), "aab": sb(C, F32),
    "ex": sb(C, F32), "eh": sb(C, F16), "ei": sb(C, F16), "xg0": sb(C, BF), "cos": sb(1, F32),
    "nf": sb(C, F32), "nb": sb(C, BF), "ss": sb(C, F32), "v0": sb(C, F32), "v1": sb(C, F32), "w0": sb(C, F32), "w1": sb(C, F32),
    "vx": sb(2 * C, F32), "val": sb(C, F32), "tab": sb(TOP + C, F32), "gj": sb(C, F32),
    "sf": sb(K, F32), "xs": sb(K, F32), "vo": sb(K, U16), "si": sb(K, I32), "sn": sb(K, F32), "xr": sb(K, F32),
    "pg": sb(2 * K, F32), "po": sb(2 * K, U16), "gx": sb(K, F32), "f2": sb(K, F32), "fo": sb(K, U16),
    "mf": sb(C, BF), "mw": sb(K, U16),
    "st": sb(C, F32), "su": sb(C, F32), "sg": sb(C, BF), "zm": sb(K, F32), "of": sb(K, F32),
    "sw": sb(K, U16), "sp": sb(C, BF), "sx": sb(C, BF), "yf": sb(C, BF), "yw": sb(K, U16),
    "hb": sb(4 * C, BF), "ga": sb(4 * C, BF), "fa": sb(4 * C, BF), "fm": sb(4 * C, BF), "rb": sb(4 * C, F32), "yo": sb(C, F32),
    "ps": ("psum", [128, 4096], F32),
}
for _k in range(3):
    SCRATCH["rq%d" % _k] = sb(C, MX)
    SCRATCH["rp%d" % _k] = sb(C, U8)
    SCRATCH["ra%d" % _k] = sb(K, U16)
    SCRATCH["rm%d" % _k] = sb(K, U16)
for _k in range(len(RADIX)):
    SCRATCH["xf%d" % _k] = sb(C, BF)
    SCRATCH["xw%d" % _k] = sb(K, U16)
LOADS = ["pi", "qi", "mi", "xt", "ut", "vt", "wq", "wp"]
STORES = ["oy", "oq", "occ", "oss"]
SEMAPHORES = ["v", "s", "t", "g"] + ["ld_" + a for a in LOADS] + ["st_" + a for a in STORES] + [a + b + str(k) for a in ("in", "out") for b in "qam" for k in range(3)]


def rank_program(g, core, T, topo):
    rank = T.rank_of(core)
    if rank is None:
        return
    queue = {"v": g.vector, "s": g.scalar, "t": g.tensor, "g": g, "y": g.sync}
    count, known, snap = {}, {e: {} for e in queue}, {}
    last, readers = {}, {}

    def settle(e, tokens):
        for s, n in sorted(tokens, key=lambda a: (a[0] == e, -a[1])):
            if known[e].get(s, 0) >= n: continue
            queue[e].wait_ge(T.sem[s], n)
            for a, b in list(snap.get((s, n), {}).items()) + [(s, n)]:
                known[e][a] = max(known[e].get(a, 0), b)

    def issue(n, e):
        tokens = set()
        for k in n["rd"]:
            if k in last: tokens.add(last[k])
        for k in n["wr"]:
            if k in last: tokens.add(last[k])
            tokens |= readers.get(k, set())
        settle(e, tokens)
        s = n["sem"] or e
        n["make"]().then_inc(T.sem[s], n["inc"])
        count[s] = count.get(s, 0) + n["inc"]
        token = (s, count[s])
        snap[token] = dict(known[e])
        snap[token][s] = count[s]
        for k in n["wr"]: last[k], readers[k] = token, set()
        for k in n["rd"]: readers.setdefault(k, set()).add(token)

    nodes = []

    def op(e, make, rd, wr, sem=None, inc=1, cost=TINY, lat=0.0, send=None):
        nodes.append(dict(e=e, make=make, rd=rd, wr=wr, sem=sem, inc=inc, cost=cost, lat=lat, send=send))

    V, S = g.vector, g.scalar

    def ts(out, in0, s1, s2, o0, o1, rd, wr, cost=TINY):
        if o1 is None: op("v", lambda: V.tensor_scalar(out, in0, s1, None, o0), rd, wr, cost=cost)
        else: op("v", lambda: V.tensor_scalar(out, in0, s1, s2, o0, o1), rd, wr, cost=cost)

    def tt(out, a, b, o, rd, wr, cost=TINY):
        op("v", lambda: V.tensor_tensor(out, a, b, o), rd, wr, cost=cost)

    def cp(out, a, rd, wr, cost=TINY):
        op("v", lambda: V.tensor_copy(out, a), rd, wr, cost=cost)

    def act(out, a, rd, wr, cost=GATHER, **how):
        op("s", lambda: S.activation(out, a, AF.Identity if how else AF.Copy, **how), rd, wr, cost=cost)

    def scan(out, a, b, init, o0, o1, rd, wr, cost=PLAIN):
        op("v", lambda: V.tensor_tensor_scan(out, a, b, init, o0, o1), rd, wr, cost=cost)

    def load(e, name, out, in_):
        op(e, lambda: queue[e].dma_start(out, in_), [], [name], "ld_" + name, 16, cost=0.1, lat=2.5)

    def store(e, name, out, in_, rd):
        op(e, lambda: queue[e].dma_start(out, in_), rd, [], "st_" + name, 16, cost=0.1, lat=2.5)

    def ordered():
        wrote, read, preds, succ = {}, {}, [], []
        for i, n in enumerate(nodes):
            p = set()
            for k in n["rd"]:
                if k in wrote: p.add(wrote[k])
            for k in n["wr"]:
                if k in wrote: p.add(wrote[k])
                p |= read.get(k, set())
            for k in n["wr"]: wrote[k], read[k] = i, set()
            for k in n["rd"]: read.setdefault(k, set()).add(i)
            p.discard(i)
            preds.append(p)
            succ.append([])
            for j in p: succ[j].append(i)
        rank_ = [0.0] * len(nodes)
        for i in range(len(nodes) - 1, -1, -1):
            rank_[i] = max([EAGER.get(a, 0.0) for a in nodes[i]["wr"]] + [0.0]) + nodes[i]["cost"] + nodes[i]["lat"] + max([rank_[j] + (NEAR if nodes[j]["e"] == nodes[i]["e"] else WAKE) for j in succ[i]] + [0.0])
        free, end, todo = {e: 0.0 for e in queue}, {}, [len(p) for p in preds]
        ready, open_, out = {}, [i for i in range(len(nodes)) if not preds[i]], []
        for i in open_: ready[i] = 0.0
        while open_:
            start = {i: max(ready[i], free[nodes[i]["e"]]) for i in open_}
            soon = min(open_, key=lambda i: (start[i], i))
            e = nodes[soon]["e"]
            due = [j for j in open_ if nodes[j]["e"] == e]
            i = max([j for j in due if start[j] <= start[soon] + SLACK], key=lambda j: (rank_[j], -j))
            for j in sorted(due, key=lambda j: -rank_[j]):
                if start[i] < start[j] < start[i] + nodes[i]["cost"] and rank_[j] - rank_[i] > nodes[j]["cost"] + 2 * (start[j] - start[i]) + YIELD:
                    small = [a for a in due if start[a] + nodes[a]["cost"] <= start[j] + SLACK]
                    i = max(small, key=lambda a: (rank_[a], -a)) if small else j
                    break
            free[e], end[i] = start[i] + nodes[i]["cost"], start[i] + nodes[i]["cost"] + nodes[i]["lat"]
            open_.remove(i)
            out.append((nodes[i], e, start[i]))
            for j in succ[i]:
                todo[j] -= 1
                if not todo[j]:
                    open_.append(j)
                    ready[j] = max([end[a] + (NEAR if nodes[a]["e"] == nodes[j]["e"] else WAKE) for a in preds[j]])
        return out

    def held(a, keys, out):
        scan(T[out][:], T.hc[:], a, 0.0, O.add, O.max, ["hc"] + keys, [out])
        return T[out][:, 15:C:16]

    def short(name, e="eh"):
        scan(T[e][:], T.hh[:], T[name][:], 0.0, O.add, O.max, ["hh", name], [e], HALF)
        return T[e][:, 15:C:16]

    def unwrap(name, w, e="eh"):
        ts(T[w][:], short(name, e), T.coh[:, 0:1], None, O.subtract, None, [e, "coh"], [w])

    def bank(b, n=C):
        return T.ps[:, 512 * b:512 * b + n]

    def mm(b, l, ls, a, r, rs, key=None):
        op("t", lambda: g.tensor.matmul_mx(bank(b), T[l][:, a:a + 128], T[ls][:, a:a + 128], T[r][:, 0:C], T[rs][:, 0:C], True, True),
           [r, rs] + ([key] if key else [l, ls]), ["ps%d" % b], cost=0.3)

    def quant(q, p, t, n, rd=None):
        op("v", lambda: V.quantize_mx(T[q][:, 0:n], T[p][:, 0:n], T[t][:, 0:4 * n]), rd or [t], [q, p], cost=0.32 * n / C)

    def iota(name, out, pattern, base, mul, small=True):
        cost = 0.14 + 0.002 * pattern[0][1]
        if small: op("g", lambda: g.iota(out, pattern, base, mul, allow_small_or_imprecise_dtypes=True), [], [name], cost=cost)
        else: op("g", lambda: g.iota(out, pattern, base, mul), [], [name], cost=cost)

    def send(k, kind, pairs, lat):
        peer = T.cores[rank ^ STEPS[k]]
        rid, pid = topo.addr(peer, core)
        mask, n = topo.mask(core, peer), len(topo.engines(core, peer)) * len(pairs)
        land, sent = "in%s%d" % (kind, k), "out%s%d" % (kind, k)

        def go():
            settle("g", {last[a] for a, x, b, y in pairs})
            for a, x, b, y in pairs:
                g.remote_dma(y, x, T.sem[land], T.sem[sent], pid, rid, mask)
                readers.setdefault(a, set()).add((sent, n))
                last[b] = (land, n)
            count[land] = count[sent] = n

        op("g", None, [a for a, x, b, y in pairs], [b for a, x, b, y in pairs], cost=0.3 * len(pairs), lat=lat, send=go)

    def part(name, b, a=0, z=K):
        return T[name][:, C * b + 16 * a:C * b + 16 * z]

    def share(cost, fixed, a, z):
        return fixed + (cost - fixed) * (z - a) / K

    load("y", "qi", T.qi[:], T.ql[:])
    load("s", "xt", T.xt[:], T.x[:])
    load("y", "pi", T.pi[:], T.pl[:])
    load("s", "ut", T.ut[:], T.u[:])
    load("y", "mi", T.mi[:], T.ml[:])
    load("y", "wq", T.wq[:].bitcast(dt.uint8), T.wc[:])
    load("y", "wp", T.wp[:], T.ws[:])
    load("y", "vt", T.vt[:], T.v[:])

    iota("di", T.di[:], [[1, K]], 129, -1, False)
    iota("pp", T.pp[:], [[1, 1]], 0, 1, False)
    iota("cw0", T.cw0[:], [[16, K]], 0, 0)
    iota("ou0", T.ou0[:], [[16, 8]], 0, 0, False)
    iota("cf", T.cf[:], [[1, C]], 0, 0)
    op("v", lambda: V.memset(T.one[:], 1.0), [], ["one"], cost=0.27)
    op("g", lambda: g.affine_select(T.et[:], T.one[:], [[-1, 516]], O.is_equal, 0.0, 3, 4), ["one"], ["et"], cost=1.2)
    ts(T.dm[:], T.di[:], 15, None, O.bitwise_and, None, ["di"], ["dm"])
    ts(T.ka[:], T.dm[:], 1.0, DROP, O.is_equal, O.mult, ["dm"], ["ka"])
    ts(T.kb[:], T.dm[:], 2.0, HOLD, O.is_equal, O.mult, ["dm"], ["kb"])
    tt(T.kc[:], T.ka[:, 0:16], T.kb[:, 0:16], O.add, ["ka", "kb"], ["kc"])
    ts(T.pm[:], T.pp[:], 15, None, O.bitwise_and, None, ["pp"], ["pm"])
    cp(T.pf[:], T.pm[:], ["pm"], ["pf"])
    ts(T.iw[:], T.cw0[:], 0.0, T.pf[:, 0:1], O.mult, O.add, ["cw0", "pf"], ["iw"])
    act(T.hh[:], T.kc[:].indirect(T.iw[:]), ["kc", "iw"], ["hh"], scale=2.0 ** -10)
    act(T.hc[:], T.hh[:], ["hh"], ["hc"], PLAIN, scale=2.0 ** 10)
    act(T.vx[:, 0:C], T.cf[:], ["cf"], ["vc"], PLAIN, bias=float(TOP + LEN))
    act(T.tab[:, TOP:TOP + C], T.cf[:], ["cf"], ["tc"], PLAIN, bias=float(TOP + LEN))
    ts(T.cor[:], T.pf[:], 15.0, HOLD, O.is_lt, O.mult, ["pf"], ["cor"])
    for name, scale, bias in (("cmd", 1.0, (C - 1) / 2), ("co2", 2.0, LEN), ("cov", 1.0, LEN + TOP - C), ("ctp", 1.0, LEN + TOP), ("coh", 2.0 ** -10, -MID), ("cos", 2.0 ** -10, 0)):
        act(T[name][:], T.cor[:], ["cor"], [name], TINY, scale=scale, bias=float(bias))
    act(T.cw[:], T.cw0[:], ["cw0", "pf"], ["cw"], TINY, bias=T.pf[:, 0:1])
    act(T.kx[:], T.cw[:], ["cw", "ctp"], ["kx"], TINY, bias=T.ctp[:, 0:1])
    act(T.kx2[:], T.cw[:], ["cw", "cov"], ["kx2"], TINY, bias=T.cov[:, 0:1])
    cp(T.ou[:], T.ou0[:], ["ou0"], ["ou"])

    cp(T.qw[:], T.qi[:], ["qi"], ["qw"])
    cp(T.pw[:], T.pi[:], ["pi"], ["pw"])
    act(T.qa[:], T.cf[:].indirect(T.qw[:]), ["cf", "qw"], ["qa"], bias=-float(MID))
    act(T.xf0[:], T.qa[:].indirect(T.pw[:]), ["qa", "pw"], ["xf0"])
    cp(T.mu[:], T.mi[:], ["mi"], ["mu"])
    act(T.sx[:], T.cf[:].indirect(T.mu[:]), ["cf", "mu"], ["sx"], bias=-float(MID))
    act(T.yf[:], T.sx[:].indirect(T.pw[:]), ["sx", "pw"], ["yf"])
    unwrap("yf", "mp")
    tt(T.dmw[:], T.mp[:], T.pi[:], O.subtract, ["mp", "pi"], ["dmw"])
    ts(T.muf[:], T.dmw[:], T.cor[:, 0:1], 2.0 ** -10, O.mult, O.mult, ["dmw", "cor"], ["muf"])
    tt(T.cq[:], T.pi[:], T.muf[:], O.subtract, ["pi", "muf"], ["cq"])
    for w, o, a in (("low", O.min, "zm"), ("hiw", O.max, "of")):
        tt(T[a][:], T.mp[:], T.pi[:], o, ["mp", "pi"], [a])
        cp(T[w][:], T[a][:], [a], [w])

    def ahead(k):
        unwrap("xf0", "xw0", "ei")
        send(k, "a", [("xw0", T.xw0[:], "ra%d" % k, T["ra%d" % k][:])], HOP)
        act(T.aab[:], T.xf0[:], ["xf0"], ["aab"], PLAIN, bias=float(MID + C * SEEN))
        for n, r in enumerate(RADIX[:-1]):
            cur = "xf%d" % n
            for j in range(r - 1):
                nxt = "xf%d" % (n + 1) if j == r - 2 else "xg%d" % j
                act(T[nxt][:], T[cur][:].indirect(T["xw%d" % n][:]), [cur, "xw%d" % n], [nxt])
                cur = nxt
            unwrap(cur, "xw%d" % (n + 1), "ei")

    def state(k):
        mm(4, "ur", "urp", 0, "tq", "tp")
        send(k, "q", [("tq", T.tq[:].bitcast(dt.uint8), "rq%d" % k, T["rq%d" % k][:].bitcast(dt.uint8)), ("tp", T.tp[:], "rp%d" % k, T["rp%d" % k][:])], FLIGHT)
        for b in range(4): mm(b, "eq", "ep", 128 * b, "tq", "tp", "eq%d" % b)

    quant("uq", "up", "ut", 128)
    cp(T.ur[:].bitcast(dt.uint32), T.uq[:].bitcast(dt.uint32).indirect(T.ou[:]), ["uq", "ou"], ["ur"], 0.25)
    op("s", lambda: S.activation(T.urp[:], T.up[:].indirect(T.ou[:]), AF.Copy), ["up", "ou"], ["urp"], cost=0.25)
    quant("tq", "tp", "xt", C)
    for b in range(4):
        op("v", lambda b=b: V.quantize_mx(T.eq[:, 128 * b:128 * b + 128], T.ep[:, 128 * b:128 * b + 128], T.et[:, 3 - b:515 - b]), ["et"], ["eq%d" % b], cost=0.15)
    quant("vq", "vp", "vt", 128)
    state(0)
    ahead(0)

    for k in range(len(STEPS)):
        final = k == len(STEPS) - 1
        ts(T.nf[:], bank(4), 0.0, float(LEN - C), O.is_ge, O.mult, [], ["ps4", "nf"], PLAIN)
        for h, (a, z) in enumerate(PIECES):
            tt(T.v0[:, 16 * a:16 * z], T.nf[:].indirect(T.xw0[:, a:z]), T.aab[:, 16 * a:16 * z], O.add, ["nf", "xw0", "aab"], ["v0%d" % h], share(GATHER, 0.05, a, z))
        cur, s = "v0", 1
        for n, r in enumerate(RADIX):
            for j in range(r - 1):
                for hs, (a, z) in ([("01", (0, K))] if j else zip("01", PIECES)):
                    act(T["w%d" % j][:, 16 * a:16 * z], T[cur][:, 16 * a:16 * z], [cur + h for h in hs], ["w%d%s" % (j, h) for h in hs], share(PLAIN, 0.03, a, z), bias=-float(C * s * (j + 1)))
            for j in range(r - 1):
                nxt = "vx" if (n, j) == (len(RADIX) - 1, r - 2) else "v1" if cur == "v0" else "v0"
                at = C if nxt == "vx" else 0
                for hs, (a, z) in ([("01", (0, K))] if nxt == "vx" else zip("01", PIECES)):
                    tt(T[nxt][:, at + 16 * a:at + 16 * z], T[cur][:].indirect(T["xw%d" % n][:, a:z]), T["w%d" % j][:, 16 * a:16 * z], O.min,
                       [cur + "0", cur + "1", "xw%d" % n] + ["w%d%s" % (j, h) for h in hs], [nxt + h for h in hs], share(GATHER, 0.05, a, z))
                cur = nxt
            s *= r
        act(T.ss[:], bank(4), ["vx1"], ["ps4", "ss"], PLAIN)
        for b in range(4): act(part("fa", b), bank(b), ["vx1"], ["ps%d" % b, "fa%d" % b], PLAIN, scale=32.0 if b in TURNED else 1.0)
        for b, at in enumerate((5, 6, 7, 4)):
            mm(at, "eq", "ep", 128 * b, "rq%d" % k, "rp%d" % k, "eq%d" % b)
            act(part("hb", b), bank(at), ["vx1"], ["ps%d" % at, "hb%d" % b], PLAIN, scale=0.5)
            act(T.ga[:, b:4 * C:4], part("hb", b).indirect(T["ra%d" % k][:]), ["hb%d" % b, "ra%d" % k], ["ga%d" % b])
        act(T.nb[:], T.nf[:], ["nf"], ["nb"], PLAIN, scale=1.0 / (LEN - C))
        ts(T.sf[:], short("nb"), T.cos[:, 0:1], None, O.is_equal, None, ["eh", "cos"], ["sf"])
        tt(T.xs[:], T.sf[:], T.kx[:], O.mult, ["sf", "kx"], ["xs"])
        tt(T.xr[:], T.xs[:], T.kx2[:], O.max, ["xs", "kx2"], ["xr"])
        ts(T.vo[:], T.xr[:], T.cov[:, 0:1], None, O.subtract, None, ["xr", "cov"], ["vo"])
        act(T.val[:], T.vx[:].indirect(T.vo[:]), ["vx0", "vx1", "vc", "vo"], ["val"])
        a = held(T.vx[:, C:2 * C], ["vx0", "vx1"], "ex")
        ts(T.si[:], a, T.cmd[:, 0:1], 1.0 / C, O.subtract, O.mult, ["ex", "cmd"], ["si"])
        tt(T.xr[:], a, T.xs[:], O.add, ["ex", "xs"], ["xr"])
        ts(T.sn[:], T.si[:], -float(C), float(LEN), O.mult, O.add, ["si"], ["sn"])
        tt(T.pg[:, K:2 * K], a, T.sn[:], O.add, ["ex", "sn"], ["pgb"])
        tt(T.pg[:, 0:K], T.pg[:, K:2 * K], T.xr[:], O.min, ["pgb", "xr"], ["pga"])
        tt(T.gx[:], T.pg[:, K:2 * K], T.xs[:], O.max, ["pgb", "xs"], ["gx"])
        ts(T.po[:], T.pg[:], T.cor[:, 0:1], None, O.subtract, None, ["pga", "pgb", "cor"], ["po"])
        cp(T.tab[:].indirect(T.po[:, 0:K]), T.val[:], ["po", "val", "tc", "gx"], ["tab"], SCATTER)
        tt(T.gj[:], T.tab[:].indirect(T.po[:, K:2 * K]), T.vx[:, C:2 * C], O.subtract, ["tab", "po", "vx0", "vx1"], ["gj"], GATHER)
        tt(T.f2[:], held(T.gj[:], ["gj"], "ex"), T.gx[:], O.add, ["ex", "gx"], ["f2"])
        ts(T.fo[:], T.f2[:], T.co2[:, 0:1], None, O.subtract, None, ["f2", "co2"], ["fo"])
        ts(T.mf[:], T.tab[:].indirect(T.fo[:]), float(TOP + LEN + MID), None, O.subtract, None, ["tab", "fo"], ["mf"], GATHER)
        unwrap("mf", "mw")
        send(k, "m", [("mw", T.mw[:], "rm%d" % k, T["rm%d" % k][:])], HOP)
        pick = act if final else cp
        pick(T.st[:], T.ss[:].indirect(T.mw[:]), ["ss", "mw"], ["st"], GATHER)
        pick(T.su[:], T.st[:].indirect(T.low[:]), ["st", "low"], ["su"], GATHER)
        tt(T.sg[:], T.st[:].indirect(T.hiw[:]), T.su[:], O.is_lt, ["st", "hiw", "su"], ["sg"], GATHER)
        tt(T.zm[:], short("sg"), T.dmw[:], O.mult, ["eh", "dmw"], ["zm"])
        tt(T.of[:], T.zm[:], T.cq[:], O.add, ["zm", "cq"], ["of"])
        cp(T.sw[:], T.of[:], ["of"], ["sw"])
        pick(T.yf[:], T.qa[:].indirect(T.sw[:]), ["qa", "sw"], ["yf"], GATHER)
        act(T.sp[:], T.cf[:].indirect(T.sw[:]), ["cf", "sw"], ["sp"], bias=-float(MID))
        act(T.sx[:], T.sp[:].indirect(T.pw[:]), ["sp", "pw"], ["sx"])
        unwrap("yf", "yw")
        act(T.xf0[:], T.sx[:].indirect(T.yw[:]), ["sx", "yw"], ["xf0"])
        if final:
            act(T.su[:], T.xf0[:].indirect(T.pw[:]), ["xf0", "pw"], ["su"], bias=float(MID))
            store("y", "oq", T.qo[:], T.su[0:128:16, :], ["su"])
        else:
            act(T.qa[:], T.xf0[:].indirect(T.pw[:]), ["xf0", "pw"], ["qa"])
            ahead(k + 1)
        for h, (a, z) in enumerate(PIECES):
            for b in range(4):
                tt(T.zt[:, 64 * a + b:64 * z:4], part("hb", b).indirect(T["rm%d" % k][:, a:z]), T.ga[:, 64 * a + b:64 * z:4], O.add, ["hb%d" % b, "rm%d" % k, "ga%d" % b], ["zt%d%d" % (b, h)], share(GATHER, 0.05, a, z))
            op("v", lambda a=a, z=z: V.quantize_mx(T.zq[:, 16 * a:16 * z], T.zp[:, 16 * a:16 * z], T.zt[:, 64 * a:64 * z]), ["zt%d%d" % (b, h) for b in range(4)], ["zq%d" % h], cost=share(0.32, 0.02, a, z))
            for b in TURNED + FUSED:
                op("t", lambda a=a, z=z, b=b, h=h: g.tensor.matmul_mx(bank(4 * h + b, 16 * (z - a)), T.wq[:, 128 * b:128 * b + 128], T.wp[:, 128 * b:128 * b + 128], T.zq[:, 16 * a:16 * z], T.zp[:, 16 * a:16 * z], True, True),
                   ["wq", "wp", "zq%d" % h], ["ps%d" % (4 * h + b)], cost=share(0.3, 0.02, a, z))
        for b in TURNED: act(part("fm", b), part("fa", b).indirect(T.mw[:]), ["fa%d" % b, "mw"], ["fm%d" % b])
        for h, (a, z) in enumerate(PIECES):
            for b in FUSED:
                act(part("rb", b, a, z), bank(4 * h + b, 16 * (z - a)), [], ["ps%d" % (4 * h + b), "rb%d%d" % (b, h)], share(PLAIN, 0.03, a, z), scale=0.03125)
            for b in TURNED:
                tt(part("rb", b, a, z), bank(4 * h + b, 16 * (z - a)), part("fm", b, a, z), O.add, ["fm%d" % b], ["ps%d" % (4 * h + b), "rb%d%d" % (b, h)], share(PLAIN, 0.03, a, z))
        for b in FUSED:
            tt(T.xt[:, b:4 * C:4], part("rb", b).indirect(T.mw[:]), part("fa", b), O.add, ["rb%d0" % b, "rb%d1" % b, "mw", "fa%d" % b], ["xt%d" % b], GATHER)
        for b in TURNED:
            act(T.xt[:, b:4 * C:4], part("rb", b).indirect(T.mw[:]), ["rb%d0" % b, "rb%d1" % b, "mw"], ["xt%d" % b], scale=0.03125)
        quant("tq", "tp", "xt", C, ["xt", "xt0", "xt1", "xt2", "xt3"])
        if not final:
            state(k + 1)
        else:
            mm(4, "vq", "vp", 0, "tq", "tp")
            store("y", "occ", T.oc[:], T.tq[:].bitcast(dt.uint8), ["tq"])
            for a in range(4): store("y" if a < 2 else "s", "oss", T.osc[4 * a:4 * a + 4, :], T.tp[32 * a:32 * a + 4, :], ["tp"])
            act(T.yo[:], bank(4), [], ["ps4", "yo"], PLAIN)
            store("s", "oy", T.y[:], T.yo[:], ["yo"])
    for n, e, t in ordered():
        if n["send"]: n["send"]()
        else: issue(n, e)
    settle("g", set(count.items()))
